import numpy as np, ml_dtypes
CORES = [35,38,43,46]
N = 4
BF = ml_dtypes.bfloat16
def gentries(a):
    return np.ascontiguousarray(a.reshape(8, 16, -1).transpose(0, 2, 1)).reshape(8, -1)
def gtable(e):
    e = np.asarray(e); return np.ascontiguousarray(e.reshape(8, -1, 16).transpose(0, 2, 1)).reshape(128, -1).astype(np.int32)
I, L, S, T, H, R = 3136, 256, 4, 4, 12, 3
M = L // S
W = I + R * (L + M)
def pack(F, sel, P):
    return {"front": np.ascontiguousarray(F.reshape(N, 128, I)).astype(np.float32).astype(BF), "sel0": np.ascontiguousarray(sel).astype(np.int32), "par": np.stack([gtable(a.reshape(8, -1)) for a in P])}
def rows8(rng):
    return (np.argsort(rng.random((8, 16)), axis=1) < 8)[None, :, :, None]
def of_class(rng, cl, want, n):
    order = np.argsort(cl + 0.5 * rng.random(cl.shape), axis=-1)
    cnt = np.stack([np.add.reduce((cl == c).astype(np.int64), axis=-1) for c in range(n)], axis=-1)
    first = np.add.accumulate(cnt, axis=-1) - cnt; w = want.reshape(N, 8, -1)
    at = np.take_along_axis(first, w, 2) + (np.take_along_axis(cnt, w, 2) * rng.random(w.shape)).astype(np.int64)
    return np.take_along_axis(order, np.minimum(at, I - 1), 2).reshape(want.shape)
def setup_inputs(rng):
    hi = rows8(rng); share = rng.choice(np.array([0.06, 0.12, 0.2]), (N, 8, 1))
    cl = np.where(rng.random((N, 8, I)) < share, 0, 1 + rng.integers(0, 2, (N, 8, I)))
    u = rng.random((N, 8, 16, I)); c = cl[:, :, None, :]
    F = np.where((c > 0) & ((c == 1) == hi), 128 + 128 * u, np.where(c == 0, 64 * u, 101 * u)).astype(np.int64)
    y = rng.random((N, 8, I)); sel = of_class(rng, cl, np.where((cl == 0) | (y < 0.15), 0, np.where(y < 0.2, 3 - cl, cl)), 3)
    free = rng.permutation(8) < 2; F = np.where(free[None, :, None, None], (256 * u).astype(np.int64), F)
    return pack(F, sel, rng.integers(0, I, (N, 8, L, 16)))
def setup_inputs_spread(rng):
    a = np.exp2(8 * rng.random((N, 8, 16, I))); b = np.exp2(8 * rng.random((N, 8, 1, I))) * rng.random((N, 8, 16, I))
    even = (rng.permutation(8) < 5)[None, :, None, None]
    F = np.minimum(np.where(even, a, b).astype(np.int64), 255) * (rng.random((N, 8, 1, I)) > 0.0625)
    low = (rng.permutation(8) < 4)[None, :, None]
    v = (I * rng.random((N, 8, I)) ** 3).astype(np.int64); sel = np.where(low, v, I - 1 - v)
    w = (I * rng.random((N, 8, L, 16)) ** 2).astype(np.int64); P = np.where(low[..., None], I - 1 - w, w)
    return pack(F, sel, P)
def setup_inputs_ends(rng):
    hi = rows8(rng); up = np.where(hi, np.add.accumulate(hi.astype(np.int64), axis=2), np.add.accumulate((~hi).astype(np.int64), axis=2)) - 1
    cl = rng.choice(np.array([0, 1, 1, 1, 2, 2, 2]), (N, 8, I))
    cl[..., [0, 1]] = 2; cl[..., I - 1] = 1; cl[..., [2, 3, I - 2]] = 3; cl[..., [4, 5, I - 3]] = 0
    off = rng.integers(0, 8, (2, N, 8, 1, I)); off[..., [0, 1, I - 1]] = 8; c = cl[:, :, None, :]
    F = 255 * ((c == 3) | ((c > 0) & ((c == 1) == hi) & (up != off[0]) & (up != off[1]))).astype(np.int64)
    F[..., 1] = np.where((~hi & (up == 7))[..., 0], 254, F[..., 1]); F[:, :, 15, 3] = 254
    for g in range(8): F[:, g, 2 * g + 1, 5] = 1
    sel = np.where(rng.random((N, 8, I)) < 0.75, (I - 1) * rng.integers(0, 2, (N, 8, I)), rng.integers(0, I, (N, 8, I)))
    cross = rng.random((N, 8)) < 0.3; cross[0, 0] = False; cross[N - 1, 7] = False; cross[0, 7] = True
    sel[..., 0] = np.where(cross, I - 1, 0); sel[..., I - 1] = np.where(cross, 0, I - 1); sel[..., 1] = 1
    inner = of_class(rng, cl, rng.choice(np.array([0, 1, 1, 1, 2, 2, 2]), (N, 8, L, 16)), 4)
    P = np.where(rng.random((N, 8, L, 16)) < 0.75, np.where(rng.random((N, 8, L, 16)) < rng.random((N, 8, L, 1)), I - 1, 0), inner)
    P[:, :, L - 1] = 1; P[:, :, L - 1, 15] = I - 1; P[:, :, 0] = 1; P[:, :, 0, 8] = I - 1
    P[:, :, L - 2] = 3; P[:, :, L - 2, 12:14] = 0
    P[:, ::2, L - 2, 5] = 2; P[:, ::2, L - 2, 10] = I - 2; P[:, 1::2, L - 2, 5] = I - 2; P[:, 1::2, L - 2, 10] = 2; P[:, :, L - 2, 15] = I - 2
    P[:, :, L - 3] = 4; P[:, :, L - 3, ::3] = I - 3
    P[:, :, L - 4] = 4; P[:, :, L - 4, 3] = 5; P[:, :, L - 4, 15] = 5
    P[::2, :, S] = 4; P[::2, :, S, ::3] = I - 3
    P[1::2, :, S] = 3; P[1::2, :, S, 9] = 2; P[1::2, :, S, 12] = I - 2
    return pack(F, sel, P)
def setup_inputs_corners(rng):
    n = T + 3; hi = rows8(rng); cl = np.argsort(rng.random((N, 8, I)), axis=-1) % n
    u = rng.random((N, 8, 16, I)); c = cl[:, :, None, :]; tall = c == T + 2
    F = np.where(c == 0, 8 * u, np.where(tall == hi, np.where(tall, 208 + 48 * u, 128 + 32 * u), np.where(tall, 8 + 33 * u, 41 * u))).astype(np.int64)
    own = np.arange(I)[None, None, :]; z = rng.integers(0, 3, (N, 8, I)); step = of_class(rng, cl, np.maximum(np.minimum(cl, T) - 1, 0), n)
    sel = np.where(cl == T + 1, own, np.where((cl == 0) | (cl == T + 2), np.where(z == 0, own, np.where(z == 1, 0, I - 1)), step))
    fm = rng.integers(0, 12, (N, 8, 1)); fm[0, 0] = 2; fm[N - 1, 7] = 1; fm[0, 7] = 6; fm[N - 1, 0] = 2; fm[1, 3] = 4; fm[2, 5] = 7
    md = np.where(fm < 6, fm, rng.integers(0, 6, (N, 8, L)))[..., None]
    one = np.arange(16) == rng.integers(0, 16, (N, 8, L, 1)); dd = rng.integers(0, T + 1, (N, 8, L, 1)); mix = rng.integers(0, n, (N, 8, L, 16))
    want = np.where(md == 0, mix, np.where(md == 1, T + 2, np.where(md == 2, np.where(one, T + 2, T + 1), np.where(md == 3, np.where(one, mix, T + 2), np.where(md == 4, np.where(one, T + 2, dd), T + 1)))))
    P = of_class(rng, cl, want, n); P = np.where(md == 1, P[..., :1], P)
    P[:, ::2, 1] = 0; P[:, 1::2, L - 1] = I - 1
    return pack(F, sel, P)
def setup_inputs_ties(rng):
    kind = rng.choice(np.array([0, 1, 1, 2, 2, 3, 4]), (N, 8, I)); rk = np.argsort(rng.random((N, 8, 16, I), dtype=np.float32), axis=2)
    more = np.array([0, 16 - H, 17 - H, 3, 0])[kind][:, :, None, :]; less = np.array([16, 16 - H, 17 - H, 13, 8])[kind][:, :, None, :]
    F = rng.integers(100, 200, (1, 8, 16, 1)) + (rk < more).astype(np.int64) - (rk >= less).astype(np.int64)
    two = rng.permutation(8)[:2]; x = int(rng.integers(0, N))
    for r in (x, (x - 1) % N):
        F[r, two[0]] += 20; F[r, two[1]] += 20
        v = rng.permutation(I)[:I // 16]; F[r, two[1], rng.integers(0, 16, v.size), v] = 0
    return pack(F, rng.integers(0, I, (N, 8, I)), rng.integers(0, I, (N, 8, L, 16)))
def check_inputs(d):
    bad = []
    for k, hi in (("front", 255), ("sel0", I - 1), ("par", I - 1)):
        x = np.asarray(d[k]).astype(np.float64)
        if not (np.min(x) >= 0 and np.max(x) <= hi): bad.append("range of " + k)
        elif np.any(x != np.floor(x)): bad.append("whole numbers in " + k)
    return bad
def reference(front, sel0, par):
    F = np.zeros((N, 8, 16, W), np.int32); F[..., :I] = front.astype(np.float32).reshape(N, 8, 16, I).astype(np.int32)
    sel = np.zeros((N, 8, W), np.int64); sel[..., :I] = sel0
    P = np.stack([gentries(a) for a in par]).astype(np.int64).reshape(N, 8, L, 16)
    i = np.arange(L); k = np.arange(16)
    def fronts(q):
        return np.take_along_axis(F, q.reshape(N, 8, 1, L * 16), 3).reshape(N, 8, 16, L, 16)
    for t in range(R):
        b = I + t * (L + M)
        f = fronts(P); s = np.argmax(np.add.reduce(f, axis=2), axis=3)
        ps = np.take_along_axis(P, s[..., None], 3)[..., 0]; g = np.take_along_axis(F, ps[:, :, None, :], 3)
        q = P; c = np.zeros(P.shape, np.int64); walk = np.ones(P.shape, bool)
        for test in range(T):
            fq = f if test == 0 else fronts(q)
            walk = walk & (np.add.reduce((fq <= g[..., None]).astype(np.int32), axis=2) < H)
            c = c + walk.astype(np.int64)
            q = np.where(walk, np.take_along_axis(sel, q.reshape(N, 8, L * 16), 2).reshape(q.shape), q)
        red = c == T
        new = np.maximum.reduce(fronts(np.where(red, ps[..., None], q)), axis=4)
        new[:, :, (i + t) & 15, i] = np.minimum(255, new[:, :, (i + t) & 15, i] + 1)
        come = np.roll(new[..., ::S], 1 + t % (N - 1), axis=0)
        best = np.argmax(np.add.reduce((f[:, :, :, ::S] <= come[..., None]).astype(np.int32), axis=2), axis=3)
        F[..., b:b + L] = new; F[..., b + L:b + L + M] = come
        sel[..., b:b + L] = ps; sel[..., b + L:b + L + M] = np.take_along_axis(P[:, :, ::S], best[..., None], 3)[..., 0]
        sc = np.add.reduce(c, axis=3)[..., None]; reds = np.add.reduce(red.astype(np.int64), axis=(1, 3))[:, None, :, None]
        P = np.where(k == s[..., None], b + i[:, None], np.where(red, b + ((5 * i[:, None] + 37 * k + sc + reds) & (L - 1)), np.where(c == 0, b + L + ((i[:, None] + k + reds) & (M - 1)), q)))
    return {"yf": np.ascontiguousarray(F[..., I:]).reshape(N, 128, W - I).astype(np.float32).astype(BF), "ys": np.ascontiguousarray(sel[..., I:]).astype(np.float32),
            "yp": np.ascontiguousarray(P.transpose(0, 1, 3, 2)).reshape(N, 128, L).astype(np.float32)}

@@ -1,0 +1,445 @@
+import numpy as np
+from concourse.bass import DstId, RemoteDMATransfer
+from concourse.mybir import dt, AluOpType, AxisListType, ActivationFunctionType
+
+OP = AluOpType
+AF = ActivationFunctionType
+SCRATCH = {}
+for _n, _c, _d in (
+        ("F", 4112, "bfloat16"), ("S", 4112, "bfloat16"), ("SELw", 3152, "bfloat16"), ("C1", 3152, "bfloat16"), ("C2", 3152, "bfloat16"),
+        ("f0", 4096, "bfloat16"), ("f1", 4096, "bfloat16"), ("Sg", 4096, "bfloat16"), ("le", 16384, "bfloat16"), ("ler", 1024, "bfloat16"),
+        ("Gb", 256, "bfloat16"), ("Gr", 2048, "bfloat16"), ("Sgs", 320, "bfloat16"), ("QL", 768, "uint16"), ("Rl", 1024, "float32"),
+        ("X", 1024, "float32"), ("X2", 512, "float32"), ("X3", 256, "float32"), ("XI", 256, "int32"), ("CI", 256, "int32"),
+        ("cb", 256, "bfloat16"), ("VT", 1024, "int32"), ("MK", 1024, "bfloat16"), ("PRD", 1024, "float32"), ("RI", 512, "int32"),
+        ("PL", 256, "uint16"), ("Pf", 256, "float32"), ("QE", 256, "uint16"), ("H", 2048, "bfloat16"), ("AC", 2048, "bfloat16"),
+        ("A2", 1024, "bfloat16"), ("A3", 512, "bfloat16"), ("A4", 256, "bfloat16"), ("A5", 256, "bfloat16"),
+        ("NF0", 64, "bfloat16"), ("NF1", 64, "bfloat16"), ("NF2", 64, "bfloat16"), ("RV0", 64, "bfloat16"), ("RV1", 64, "bfloat16"), ("RV2", 64, "bfloat16"),
+        ("Mm", 40, "int32"), ("mi", 40, "int32"), ("L1", 40, "uint16"), ("mb", 32, "bfloat16"),
+        ("sl", 196, "int32"), ("slf", 196, "float32"), ("slh", 196, "bfloat16"), ("sll", 196, "bfloat16"), ("LS", 200, "uint16"),
+        ("iu", 144, "float32"), ("ib", 128, "float32"), ("i16", 8, "float32"), ("pi", 1, "int32"), ("pii", 4, "int32"), ("pc", 16, "float32"),
+        ("Ib", 128, "bfloat16"), ("If", 128, "float32"), ("GA", 128, "bfloat16"), ("Sh", 128, "bfloat16"), ("In", 128, "bfloat16"),
+        ("BI", 768, "bfloat16"), ("Z0", 144, "bfloat16"), ("Z1", 144, "bfloat16"), ("Z2", 144, "bfloat16"), ("Z3", 144, "bfloat16"),
+        ("K63", 64, "bfloat16"), ("Zh", 144, "bfloat16"), ("C512", 64, "bfloat16"), ("half", 1, "float32"), ("OFF", 192, "bfloat16"), ("ki", 768, "int32"), ("ki2", 768, "int32"), ("ki3", 768, "int32"), ("KB", 512, "bfloat16"),
+        ("gi", 384, "int32"), ("gi2", 384, "int32"), ("GM", 384, "bfloat16"), ("Ys", 8, "bfloat16"),
+        ("T1", 512, "bfloat16"), ("T2", 512, "bfloat16"), ("T3", 512, "bfloat16"), ("T4", 512, "bfloat16"), ("XT", 512, "bfloat16"),
+        ("bi", 16, "float32"), ("bc", 16, "float32")):
+    SCRATCH[_n] = ("sbuf", [128, _c], _d)
+SCRATCH["PS"] = ("sbuf", [64, 512], "int32")
+SCRATCH["PSf"] = ("sbuf", [64, 512], "float32")
+SCRATCH["PT"] = ("sbuf", [64, 512], "float32")
+SCRATCH["FT"] = ("sbuf", [64, 1024], "bfloat16")
+SCRATCH["Rk"] = ("sbuf", [64, 64], "bfloat16")
+SCRATCH["irk"] = ("sbuf", [64, 64], "float32")
+SCRATCH["mT"] = ("sbuf", [4, 512], "bfloat16")
+SCRATCH["SS"] = ("sbuf", [49, 512], "int32")
+SCRATCH["SSf"] = ("sbuf", [49, 512], "float32")
+SCRATCH["ysb"] = ("sbuf", [8, 960], "float32")
+for _k in range(8):
+    SCRATCH["b%d" % _k] = ("psum", [128, 512], "float32")
+GROUPS = ["dpar", "dsel", "dsl", "dfr", "dsw", "ds1", "ds2", "ds3", "doutf", "douts", "doutp"]
+SEMAPHORES = ["sV", "sA", "sP", "sG", "rv0", "rv1", "rv2", "ls"] + GROUPS
+ENG = ("V", "A", "P", "G", "Y")
+SIGN = (0, 1)
+GAM = 1.56
+CY = 0.00104
+
+
+def rank_program(g, core, T, topo):
+    rank = T.rank_of(core)
+    if rank is None:
+        return
+    ops = []
+    early = [0.0]
+    lastw, readers, psum = {}, {}, {}
+
+    def op(eng, fn, r=(), w=(), d=0.1, ps=(), grp=None, bias=0.0):
+        k = len(ops)
+        hard, soft = set(), set()
+        for x in r:
+            if x in lastw: hard.add(lastw[x])
+        for x in w:
+            if x in lastw: hard.add(lastw[x])
+            soft |= readers.get(x, set())
+        for x in r: readers.setdefault(x, set()).add(k)
+        for x in w: lastw[x] = k; readers[x] = set()
+        for b in ps:
+            runs = psum.setdefault(b, [])
+            if not runs or runs[-1][0] != eng: runs.append((eng, []))
+            runs[-1][1].append(k)
+            if len(runs) > 1: hard |= set(runs[-2][1])
+        hard.discard(k); soft.discard(k)
+        ops.append({"e": eng, "f": fn, "h": hard, "s": soft - hard, "d": d, "g": grp, "b": bias + early[0]})
+        return k
+
+    V, A, TE = g.vector, g.scalar, g.tensor
+
+    def vd(n, c=1.0): return max(64, n * c) * CY + 0.03
+    def gd(n): return 0.06 + n * GAM * CY
+    def ad(n): return max(64, n) * CY + 0.06
+
+    def gather(eng, out, win, off, r, w, n):
+        if eng == "V": op("V", lambda inc: inc(V.tensor_copy(out, win.indirect(off))), r, w, gd(n))
+        else: op("A", lambda inc: inc(A.activation(out, win.indirect(off), AF.Copy)), r, w, gd(n))
+
+    def ts(out, i0, s1, s2, o1, o2=None, r=(), w=(), n=64, ps=(), c=1.0):
+        if o2 is None: op("V", lambda inc: inc(V.tensor_scalar(out, i0, s1, None, o1)), r, w, vd(n, c), ps)
+        else: op("V", lambda inc: inc(V.tensor_scalar(out, i0, s1, s2, o1, o2)), r, w, vd(n, c), ps)
+
+    def tt(out, i0, i1, o, r=(), w=(), n=64, ps=()):
+        op("V", lambda inc: inc(V.tensor_tensor(out, i0, i1, o)), r, w, vd(n, 1.0 if ps else 2.0), ps)
+
+    def cp(out, i0, r=(), w=(), n=64, ps=(), c=1.0):
+        op("V", lambda inc: inc(V.tensor_copy(out, i0)), r, w, vd(n, c), ps)
+
+    def act(out, i0, r=(), w=(), n=64, ps=(), f=None, bias=0.0, scale=1.0):
+        op("A", lambda inc: inc(A.activation(out, i0, f or AF.Copy, bias=bias, scale=scale)), r, w, ad(n), ps)
+
+    def mm(groups, r=(), w=(), ps=(), n=64):
+        def fn(inc):
+            for out, prs in groups:
+                for j, (a, b) in enumerate(prs):
+                    z = TE.matmul(out, a, b, j == 0, j == len(prs) - 1)
+                inc(z)
+        op("P", fn, r, w, sum(len(p) for _, p in groups) * max(64, n) * 0.0006 + 0.1, ps)
+
+    def dma(eng, out, in_, grp, r=(), w=(), d=2.0):
+        q = {"Y": g.sync, "A": g.scalar}[eng]
+        op(eng, lambda inc: q.dma_start(out, in_).then_inc(T.sem[grp], 16), r, w, d, grp=grp)
+
+    def iota(out, pat, base, cm, w, n, flag=True):
+        if flag: op("G", lambda inc: inc(g.iota(out, pat, base, cm, allow_small_or_imprecise_dtypes=True)), (), w, 0.13 + 2 * n * CY)
+        else: op("G", lambda inc: inc(g.iota(out, pat, base, cm)), (), w, 0.13 + 2 * n * CY)
+
+    def fill(ap, c, w, n): op("V", lambda inc: inc(V.memset(ap, c)), (), w, vd(n, 0.5))
+
+    B0 = 3152
+    dma("Y", T.sl[:, :], T.sel0[:, :], "dsl", (), ("sl",))
+    for k in range(8):
+        dma("A" if k % 2 else "Y", T.PS[:, 64 * k:64 * k + 64], T.par[16 * k:16 * k + 16, :], "dpar", (), ("PS%d" % k,))
+    for k in range(8):
+        dma("A" if k % 2 else "Y", T.SS[:, 64 * k:64 * k + 64], T.sel0[k:k + 1, :], "dsel", (), ("SS%d" % k,))
+    dma("Y", T.F[:, 16:B0], T.front[:, :], "dfr", (), ("Fi",), 6.0)
+    iota(T.pi[:, :], [[0, 1]], 0, 1, ("pi",), 1, False)
+    iota(T.iu[:, :], [[1, 144]], 0, 0, ("iu",), 144)
+    iota(T.ib[:, :], [[0, 8], [1, 16]], 0, 0, ("ib",), 128)
+    iota(T.irk[:, :], [[0, 16], [1, 4]], 0, 0, ("irk",), 64)
+    iota(T.bi[:, :], [[512, 16]], 0, 0, ("bi",), 16)
+    iota(T.T1[:, :], [[16, 32], [0, 16]], 0, 0, ("T1",), 512)
+    iota(T.T2[:, :], [[0, 32], [1, 16]], 0, 0, ("T2",), 512)
+    iota(T.K63[:, :], [[-1, 64]], 63, 0, ("K63",), 64)
+    iota(T.i16[:, :], [[16, 8]], 15, 0, ("i16",), 8)
+    iota(T.ki[:, 0:256], [[1, 4], [1, 16], [64, 4]], 0, 0, ("ki0",), 256, False)
+    iota(T.ki[:, 256:512], [[5, 4], [37, 16], [320, 4]], 0, 0, ("ki1",), 256, False)
+    iota(T.ki[:, 512:768], [[1, 4], [0, 16], [64, 4]], 0, 0, ("ki2",), 256, False)
+    iota(T.gi[:, :], [[1, 6], [0, 16], [4, 4]], 0, 0, ("gi",), 384, False)
+    fill(T.F[:, 0:16], 0.0, ("Fz",), 16)
+    fill(T.SELw[:, :], 0.0, ("SELw",), 3152)
+    fill(T.C1[:, 0:16], 0.0, ("C1z",), 16)
+    for k in range(3): fill(T.OFF[:, 64 * k:64 * k + 64], 8192.0 * (k + 1), ("OFF%d" % k,), 64)
+    ts(T.pii[:, 0:1], T.pi[:, :], 15, None, OP.bitwise_and, r=("pi",), w=("pii0",))
+    ts(T.pii[:, 1:2], T.pi[:, :], 15, 1, OP.bitwise_and, OP.arith_shift_right, r=("pi",), w=("pii1",))
+    ts(T.pii[:, 2:3], T.pi[:, :], 3, None, OP.bitwise_and, r=("pi",), w=("pii2",))
+    cp(T.pc[:, 0:1], T.pi[:, :], ("pi",), ("pc0",))
+    cp(T.pc[:, 1:2], T.pii[:, 0:1], ("pii0",), ("pc1",))
+    tt(T.pc[:, 14:15], T.pc[:, 0:1], T.pc[:, 1:2], OP.subtract, ("pc0", "pc1"), ("pc14",))
+    ts(T.pc[:, 2:3], T.pc[:, 14:15], 15.0, None, OP.add, r=("pc14",), w=("pc2",))
+    ts(T.pc[:, 3:4], T.pc[:, 1:2], 1008.0, None, OP.add, r=("pc1",), w=("pc3",))
+    cp(T.pc[:, 4:5], T.pii[:, 1:2], ("pii1",), ("pc4",))
+    for k in (1, 2, 3): ts(T.pc[:, 4 + k:5 + k], T.pc[:, 4:5], float(k), None, OP.is_equal, r=("pc4",), w=("pc%d" % (4 + k),))
+    for k in (0, 1): ts(T.pc[:, 8 + k:9 + k], T.pc[:, 1:2], float(k), None, OP.is_equal, r=("pc1",), w=("pc%d" % (8 + k),))
+    ts(T.pc[:, 10:11], T.pc[:, 4:5], 3.0, None, OP.is_lt, r=("pc4",), w=("pc10",))
+    cp(T.pc[:, 11:12], T.pii[:, 2:3], ("pii2",), ("pc11",))
+    ts(T.pc[:, 12:13], T.pc[:, 1:2], 20.0, None, OP.mult, r=("pc1",), w=("pc12",))
+    ts(T.pc[:, 13:14], T.pc[:, 1:2], 4.0, None, OP.mult, r=("pc1",), w=("pc13",))
+    ts(T.pc[:, 15:16], T.pc[:, 0:1], 2.0, None, OP.add, r=("pc0",), w=("pc15",))
+    ts(T.If[:, :], T.iu[:, 0:128], T.pc[:, 0:1], None, OP.is_equal, r=("iu", "pc0"), w=("If",), n=128)
+    ts(T.Ib[:, :], T.iu[:, 0:128], T.pc[:, 0:1], None, OP.is_equal, r=("iu", "pc0"), w=("Ib",), n=128)
+    ts(T.Z0[:, :], T.iu[:, :], T.pc[:, 2:3], 64.0, OP.is_equal, OP.mult, r=("iu", "pc2"), w=("Z0",), n=144)
+    ts(T.Zh[:, :], T.Z0[:, :], 0.5, None, OP.mult, r=("Z0",), w=("Zh",), n=144, c=0.5)
+    fill(T.C512[:, :], 512.0, ("C512",), 64)
+    fill(T.half[:, :], 0.5, ("half",), 1)
+    for k in (1, 2, 3):
+        ts(T["Z%d" % k][:, :], T.iu[:, :], T.pc[:, 2:3], T.pc[:, 4 + k:5 + k], OP.is_equal, OP.mult, r=("iu", "pc2", "pc%d" % (4 + k)), w=("Z%d" % k,), n=144)
+    ts(T.GA[:, :], T.ib[:, :], T.pc[:, 1:2], None, OP.is_equal, r=("ib", "pc1"), w=("GA",), n=128)
+    ts(T.Sh[:, :], T.iu[:, 0:128], T.pc[:, 15:16], T.pc[:, 10:11], OP.is_equal, OP.mult, r=("iu", "pc15", "pc10"), w=("Sh",), n=128)
+    ts(T.In[:, :], T.Ib[:, :], -1.0, None, OP.mult, r=("Ib",), w=("In",), n=128, c=0.5)
+    for k in range(3):
+        ts(T.BI[:, 256 * k:256 * k + 128], T.Ib[:, :], float(B0 + 320 * k), None, OP.mult, r=("Ib",), w=("BIa%d" % k,), n=128, c=0.5)
+        ts(T.BI[:, 256 * k + 128:256 * k + 256], T.Ib[:, :], float(B0 + 320 * k + 256), None, OP.mult, r=("Ib",), w=("BIb%d" % k,), n=128, c=0.5)
+    ts(T.Rk[:, :], T.irk[:, :], T.pc[0:64, 11:12], None, OP.is_equal, r=("irk", "pc11"), w=("Rk",))
+    ts(T.Ys[:, :], T.i16[:, :], T.pc[:, 2:3], T.pc[:, 5:6], OP.is_equal, OP.mult, r=("i16", "pc2", "pc5"), w=("Ys",))
+    ts(T.ki2[:, 0:256], T.ki[:, 0:256], T.pc[:, 13:14], None, OP.add, r=("ki0", "pc13"), w=("kj0",), n=256)
+    ts(T.ki2[:, 256:512], T.ki[:, 256:512], T.pc[:, 12:13], None, OP.add, r=("ki1", "pc12"), w=("kj1",), n=256)
+    ts(T.ki3[:, 0:256], T.ki2[:, 0:256], 63, None, OP.bitwise_and, r=("kj0",), w=("kk0",), n=256)
+    ts(T.ki3[:, 256:512], T.ki2[:, 256:512], 255, None, OP.bitwise_and, r=("kj1",), w=("kk1",), n=256)
+    for r in range(4):
+        cp(T.KB[:, 128 * r:128 * r + 64], T.ki3[:, 64 * r:64 * r + 64], ("kk0",), ("KBa%d" % r,))
+        cp(T.KB[:, 128 * r + 64:128 * r + 128], T.ki3[:, 256 + 64 * r:320 + 64 * r], ("kk1",), ("KBb%d" % r,))
+        ts(T.VT[:, 256 * r + 192:256 * r + 256], T.ki[:, 512 + 64 * r:576 + 64 * r], T.pc[:, 13:14], None, OP.add, r=("ki2", "pc13"), w=("VTi%d" % r,))
+    ts(T.gi2[:, :], T.gi[:, :], 15, None, OP.bitwise_and, r=("gi",), w=("gi2",), n=384)
+    ts(T.GM[:, :], T.gi2[:, :], T.pc[:, 1:2], None, OP.is_equal, r=("gi2", "pc1"), w=("GM",), n=384)
+    early[0] = 30.0
+    ts(T.T3[:, :], T.T1[:, :], T.pc[:, 8:9], None, OP.mult, r=("T1", "pc8"), w=("T3",), n=512, c=0.5)
+    ts(T.T4[:, :], T.T2[:, :], T.pc[:, 9:10], None, OP.mult, r=("T2", "pc9"), w=("T4",), n=512, c=0.5)
+    tt(T.XT[:, :], T.T3[:, :], T.T4[:, :], OP.add, ("T3", "T4"), ("XT",), 512)
+    ts(T.bc[:, :], T.bi[:, :], T.pc[:, 8:9], None, OP.mult, r=("bi", "pc8"), w=("bc",))
+    for k in range(9):
+        e = min(4112, 512 * k + 512)
+        act(T.S[:, 512 * k:e], T.XT[:, 0:e - 512 * k], ("XT", "bc"), ("Sv%d" % k,), 512, f=AF.Identity, bias=T.bc[:, k:k + 1])
+    Sv = tuple("Sv%d" % k for k in range(9))
+    early[0] = 0.0
+    ts(T.PSf[:, :], T.PS[:, :], 16.0, None, OP.add, r=tuple("PS%d" % k for k in range(8)), w=("PSf",), n=512)
+    mm([(T.b6[:, 64 * r:64 * r + 64], [(T.PSf[:, r::4], T.If[0:64, 0:64])]) for r in range(4)], ("PSf", "If"), (), ("b6",), 256)
+    cp(T.PL[:, :], T.b6[:, 0:256], (), tuple("PL%d" % r for r in range(4)), 256, ("b6",))
+    act(T.Pf[:, :], T.b6[:, 0:256], (), tuple("Pf%d" % r for r in range(4)), 256, ("b6",))
+    ts(T.SSf[:, :], T.SS[:, :], 16.0, None, OP.add, r=tuple("SS%d" % k for k in range(8)), w=("SSf",), n=512)
+    mm([(T.b5[:, 50 * r:50 * r + 49], [(T.SSf[:, r::4], T.If[0:49, 0:49])]) for r in range(4)], ("SSf", "If"), (), ("b5",), 256)
+    for r in range(4): cp(T.LS[:, 50 * r:50 * r + 49], T.b5[:, 50 * r:50 * r + 49], (), ("LS%d" % r,), 64, ("b5",))
+    ts(T.slf[:, :], T.sl[:, :], 16.0, None, OP.add, r=("sl",), w=("slf",), n=196)
+    cp(T.slh[:, :], T.slf[:, :], ("slf",), ("slh",), 196)
+    tt(T.sll[:, :], T.slf[:, :], T.slh[:, :], OP.subtract, ("slf", "slh"), ("sll",), 196)
+    dma("Y", T.SELw[2::16, 16:B0], T.slh[:, :], "dsw", ("slh", "SELw"), ("SW2",))
+    dma("Y", T.SELw[3::16, 16:B0], T.sll[:, :], "dsw", ("sll", "SELw"), ("SW3",))
+    for r in range(4):
+        gather("VA"[r % 2], T.C1[:, 16 + r:B0:4], T.SELw[:, :], T.LS[:, 50 * r:50 * r + 49], ("SELw", "SW2", "SW3", "LS%d" % r), ("C1%d" % r,), 784)
+    c1 = ("C1z",) + tuple("C1%d" % r for r in range(4))
+    for r in range(4):
+        gather("VA"[r % 2], T.C2[:, 16 + r:B0:4], T.C1[:, :], T.LS[:, 50 * r:50 * r + 49], c1 + ("LS%d" % r,), ("C2%d" % r,), 784)
+    c2 = tuple("C2%d" % r for r in range(4))
+    for k in (0, 1):
+        dma("Y", T.S[2 + k::16, 16:B0], T.SELw[2 + k::16, 16:B0], "ds1", ("SW2", "SW3") + Sv, ("S%d" % (2 + k),))
+    for k in (0, 1):
+        dma("Y", T.S[4 + k::16, 16:B0], T.C1[2 + k::16, 16:B0], "ds2", c1 + Sv, ("S%d" % (4 + k),))
+    for k in (0, 1):
+        dma("Y", T.S[6 + k::16, 16:B0], T.C2[2 + k::16, 16:B0], "ds3", c2 + Sv, ("S%d" % (6 + k),))
+    Sr = Sv + tuple("S%d" % k for k in range(2, 8))
+    Fr = ("Fi", "Fz")
+
+    def z(n, y): return T["Z%s" % n][:, 15 - y:143 - y]
+
+    def key(src, rk, n):
+        mm([(T.b0[:, 0:64], [(z(0, y), src[:, y::16]) for y in range(16)] + [(T.Ib[:, :], T.K63[:, :])])], rk + ("Z0", "Ib", "K63"), (), ("b0",))
+        for c in range(4):
+            op("V", lambda inc, c=c: inc(V.tensor_reduce(T.Mm[:, 8 * n + c:8 * n + c + 1], T.b0[:, c:64:4], AxisListType.X, OP.max)), (), ("Mm%d%d" % (n, c),), vd(64), ("b0",))
+        ts(T.mi[:, 8 * n:8 * n + 4], T.Mm[:, 8 * n:8 * n + 4], 63, None, OP.bitwise_and, r=tuple("Mm%d%d" % (n, c) for c in range(4)), w=("mi%d" % n,))
+        ts(T.L1[:, 8 * n:8 * n + 4], T.mi[:, 8 * n:8 * n + 4], -16.0, T.pc[:, 3:4], OP.mult, OP.add, r=("mi%d" % n, "pc3"), w=("L1%d" % n,))
+        return T.L1[:, 8 * n:8 * n + 4]
+
+    def newsel(n, r, sv, cols, w):
+        mm([(T.b7[:, 0:64], [(T.Sh[:, :], T.Sgs[:, 64 * n:64 * n + 64]), (T.Ib[:, :], cols)])], ("Sgs%d" % n, "Sh", "Ib") + Sv, (), ("b7",))
+        act(cols, T.b7[:, 0:64], (), w, 64, ("b7",))
+
+    for t in range(3):
+        B = B0 + 320 * t
+        win, swin = T.F[:, 0:B], T.S[:, 0:B]
+        fin = ()
+        for r in range(4):
+            q0, q4 = 64 * r, 256 * r
+            Q, GP = T["b%d" % (1 + r % 2)], T["b%d" % (3 + r % 2)]
+            Qb, GPb = "b%d" % (1 + r % 2), "b%d" % (3 + r % 2)
+            R = "%d" % r
+            PL, Pf = T.PL[:, q0:q0 + 64], T.Pf[:, q0:q0 + 64]
+            f0, f1, Sg = T.f0[:, 1024 * r:1024 * r + 1024], T.f1[:, 1024 * r:1024 * r + 1024], T.Sg[:, 1024 * r:1024 * r + 1024]
+            gather("A", f0, win, PL, Fr + ("PL" + R,), ("f0" + R,), 1024)
+            gather("A", Sg, swin, PL, Sr + ("PL" + R,), ("Sg" + R,), 1024)
+            L1 = key(f0, ("f0" + R,), r)
+            gather("V", T.Gb[:, q0:q0 + 64], f0, L1, ("f0" + R, "L1" + R), ("Gb" + R,), 64)
+            mm([(GP[:, 64 * k:64 * k + 64], [(T.Ib[:, :], T.Gb[:, q0:q0 + 64])]) for k in range(8)], ("Gb" + R, "Ib"), (), (GPb,))
+            act(T.Gr[:, 512 * r:512 * r + 512], GP[:, :], (), ("Gr" + R,), 512, (GPb,))
+            grp = [(Q[:, 0:64], [(T.If[:, :], Pf)])]
+            for h in (1, 2, 3):
+                grp.append((Q[:, 64 * h:64 * h + 64], [(z(h, y), Sg[:, y::16]) for y in range(16)] + [(T.Ib[:, :], T.OFF[:, 64 * h - 64:64 * h])]))
+            mm(grp, ("Pf" + R, "If", "Sg" + R, "Z1", "Z2", "Z3", "Ib", "OFF0", "OFF1", "OFF2"), (), (Qb,))
+            for h in (1, 2, 3):
+                a = 192 * r + 64 * h - 64
+                ts(T.QL[:, a:a + 64], Q[:, 64 * h:64 * h + 64], -8192.0 * h, None, OP.add, w=("QL%d%d" % (r, h),), ps=(Qb,))
+            gather("A", f1, win, T.QL[:, 192 * r:192 * r + 64], Fr + ("QL%d1" % r,), ("f1" + R,), 1024)
+            gather("V", T.Sgs[:, q0:q0 + 64], Sg, L1, ("Sg" + R, "L1" + R), ("Sgs" + R,), 64)
+            for h in range(4):
+                for b in (0, 1):
+                    le = T.le[:, 4096 * r + 1024 * h + 512 * b:4096 * r + 1024 * h + 512 * b + 512]
+                    k = ("le%d%d%d" % (r, h, b),)
+                    if h in SIGN:
+                        D, Db = T["b%d" % (3 + b)], "b%d" % (3 + b)
+                        mm([(D[:, :], [(T.In[:, :], (f0, f1)[h][:, 512 * b:512 * b + 512]), (T.Ib[:, :], T.Gr[:, 512 * r:512 * r + 512])])],
+                           ("f%d" % h + R, "Gr" + R, "In", "Ib"), (), (Db,), 512)
+                        op("A", lambda inc, le=le, D=D: inc(A.activation(le, D[:, :], AF.Sign, bias=T.half[:, :])), ("half",), k, ad(512), (Db,))
+                    elif h < 2:
+                        tt(le, (f0, f1)[h][:, 512 * b:512 * b + 512], GP[:, :], OP.is_le, ("f%d" % h + R,), k, 512, (GPb,))
+                    else:
+                        a = 192 * r + 64 * h - 64 + 32 * b
+                        op("V", lambda inc, le=le, a=a, r=r, win=win: inc(V.tensor_tensor(le, win.indirect(T.QL[:, a:a + 32]), T.Gr[:, 512 * r:512 * r + 512], OP.is_le)),
+                           Fr + ("QL%d%d" % (r, h), "Gr" + R), k, gd(512))
+                lh = 4096 * r + 1024 * h
+                sg = h in SIGN
+                mm([(T.b5[:, 64 * h:64 * h + 64], [(z("h" if sg else 0, y), T.le[:, lh + y:lh + 1024:16]) for y in range(16)] + ([(T.Ib[:, :], T.C512[:, :])] if sg else []))],
+                   ("le%d%d0" % (r, h), "le%d%d1" % (r, h), "Z0", "Zh", "C512", "Ib"), (), ("b5",))
+            act(T.Rl[:, q4:q4 + 256], T.b5[:, 0:256], (), ("Rl" + R,), 256, ("b5",), AF.Relu, 786432.0, -1024.0)
+            tt(Q[:, 256:384], T.Rl[:, q4 + 128:q4 + 256], Q[:, 128:256], OP.add, ("Rl" + R,), ("XP" + Qb,), 128, (Qb,))
+            tt(T.X[:, q4:q4 + 128], T.Rl[:, q4:q4 + 128], Q[:, 0:128], OP.add, ("Rl" + R,), ("X" + R,), 128, (Qb,))
+            tt(Q[:, 384:448], T.X[:, q4 + 64:q4 + 128], Q[:, 320:384], OP.min, ("X" + R, "XP" + Qb), ("XQ" + Qb,), 64, (Qb,))
+            tt(T.X2[:, 128 * r:128 * r + 64], T.X[:, q4:q4 + 64], Q[:, 256:320], OP.min, ("X" + R, "XP" + Qb), ("X2" + R,), 64, (Qb,))
+            tt(T.X3[:, q0:q0 + 64], T.X2[:, 128 * r:128 * r + 64], Q[:, 384:448], OP.min, ("X2" + R, "XQ" + Qb), ("X3" + R,), 64, (Qb,))
+            ts(T.XI[:, q0:q0 + 64], T.X3[:, q0:q0 + 64], 32768.0, None, OP.min, r=("X3" + R,), w=("XI" + R,))
+            ts(T.VT[:, q4:q4 + 64], T.XI[:, q0:q0 + 64], 8191, None, OP.bitwise_and, r=("XI" + R,), w=("VTq" + R,))
+            cp(T.QE[:, q0:q0 + 64], T.VT[:, q4:q4 + 64], ("VTq" + R,), ("QE" + R,))
+            h5 = 512 * r
+            gather("A", T.H[:, h5:h5 + 512], win, T.QE[:, q0 + 32:q0 + 64], Fr + ("QE" + R,), ("H" + R,), 512)
+            op("V", lambda inc, h5=h5, q0=q0, win=win: inc(V.tensor_tensor(T.AC[:, h5:h5 + 512], win.indirect(T.QE[:, q0:q0 + 32]), T.H[:, h5:h5 + 512], OP.max)),
+               Fr + ("QE" + R, "H" + R), ("AC" + R,), gd(512))
+            tt(T.b7[:, 384:512], T.AC[:, h5 + 128:h5 + 256], T.AC[:, h5 + 384:h5 + 512], OP.max, ("AC" + R,), ("AP",), 256, ("b7",))
+            tt(T.A2[:, q4:q4 + 128], T.AC[:, h5:h5 + 128], T.AC[:, h5 + 256:h5 + 384], OP.max, ("AC" + R,), ("A2" + R,), 128)
+            tt(T.b7[:, 320:384], T.A2[:, q4 + 64:q4 + 128], T.b7[:, 448:512], OP.max, ("A2" + R, "AP"), ("AQ",), 64, ("b7",))
+            tt(T.A3[:, 128 * r:128 * r + 64], T.A2[:, q4:q4 + 64], T.b7[:, 384:448], OP.max, ("A2" + R, "AP"), ("A3" + R,), 64, ("b7",))
+            tt(T.A4[:, q0:q0 + 64], T.A3[:, 128 * r:128 * r + 64], T.b7[:, 320:384], OP.max, ("A3" + R, "AQ"), ("A4" + R,), 64, ("b7",))
+            gm = 64 * (r + t)
+            tt(T.A5[:, q0:q0 + 64], T.A4[:, q0:q0 + 64], T.GM[:, gm:gm + 64], OP.add, ("A4" + R, "GM"), ("A5" + R,), 64)
+            fk = "F%d%d" % (t, r)
+            if r == 0:
+                NF, RV = T["NF%d" % t], T["RV%d" % t]
+                ts(NF[:, :], T.A5[:, q0:q0 + 64], 255.0, None, OP.min, r=("A5" + R,), w=("NF%d" % t,), c=0.5)
+                dst = T.cores[(rank + 1 + t % 3) % 4]
+                src = T.cores[(rank - 1 - t % 3) % 4]
+                ne = topo.engines(core, dst)[:8]
+                nr = len(topo.engines(src, core)[:8])
+
+                def send(inc, t=t, dst=dst, ne=ne, NF=NF, RV=RV):
+                    rid, pid = topo.addr(dst)[:2]
+                    g.remote_dma(RV[:, :], NF[:, :], T.sem["rv%d" % t], T.sem["ls"], pid, rid, sum(1 << e for e in ne))
+                op("G", send, ("NF%d" % t,), ("sent%d" % t,), 1.5, grp="send")
+                op("N", ("rv%d" % t, nr), ("sent%d" % t,), ("RV%d" % t,), 2.5)
+                act(T.F[:, B + r:B + 256:4], NF[:, :], ("NF%d" % t,), (fk,), 64)
+            else:
+                ts(T.F[:, B + r:B + 256:4], T.A5[:, q0:q0 + 64], 255.0, None, OP.min, r=("A5" + R,), w=(fk,), c=0.5)
+            newsel(r, r, None, T.S[:, B + r:B + 256:4], ("T%d%d" % (t, r),))
+            m4 = 8 * r
+            cp(T.mb[:, m4:m4 + 4], T.mi[:, m4:m4 + 4], ("mi" + R,), ("mb" + R,))
+            mm([(T.b6[0:4, 256:384], [(T.mb[:, m4:m4 + 4], T.Ib[:, :])])], ("mb" + R, "Ib"), (), ("b6",), 128)
+            act(T.mT[:, 128 * r:128 * r + 128], T.b6[0:4, 256:384], (), ("mT" + R,), 128, ("b6",))
+            mm([(T.b6[:, 0:64], [(T.mT[:, 128 * r:128 * r + 128], T.Rk[0:4, :]), (T.In[:, :], T.K63[:, :])])], ("mT" + R, "Rk", "In", "K63"), (), ("b6",))
+            ts(T.MK[:, q4 + 192:q4 + 256], T.b6[:, 0:64], 0.0, None, OP.is_equal, w=("MKs" + R,), ps=("b6",))
+            ts(T.MK[:, q4:q4 + 64], T.X3[:, q0:q0 + 64], 8192.0, None, OP.is_ge, r=("X3" + R,), w=("MKn" + R,))
+            ts(T.MK[:, q4 + 128:q4 + 192], T.X3[:, q0:q0 + 64], 32768.0, None, OP.is_ge, r=("X3" + R,), w=("MKr" + R,))
+            ts(T.CI[:, q0:q0 + 64], T.XI[:, q0:q0 + 64], 13, None, OP.arith_shift_right, r=("XI" + R,), w=("CI" + R,))
+            cp(T.cb[:, q0:q0 + 64], T.CI[:, q0:q0 + 64], ("CI" + R,), ("cb" + R,))
+            tt(T.MK[:, q4 + 64:q4 + 128], T.MK[:, q4:q4 + 64], T.MK[:, q4 + 192:q4 + 256], OP.is_equal, ("MKn" + R, "MKs" + R), ("MK0" + R,), 64)
+            red, cb = T.MK[:, q4 + 128:q4 + 192], T.cb[:, q0:q0 + 64]
+            mm([(T.b6[0:64, 0:128], [(red, T.GA[:, :])]), (T.b6[0:64, 128:256], [(red, T.GA[:, :]), (cb, T.Ib[:, :])])], ("MKr" + R, "cb" + R, "GA", "Ib"), (), ("b6",), 128)
+            act(T.FT[:, q4:q4 + 256], T.b6[0:64, 0:256], (), ("FT" + R,), 256, ("b6",))
+            kb = 128 * r
+            mm([(T.b6[:, 256 + 64 * j:320 + 64 * j], [(T.FT[:, q4 + 128 * j:q4 + 128 * j + 128], T.Rk[:, :]), (T.Ib[:, :], T.KB[:, kb + 64 * j:kb + 64 * j + 64])]) for j in (0, 1)],
+               ("FT" + R, "Rk", "Ib", "KBa" + R, "KBb" + R), (), ("b6",))
+            cp(T.RI[:, kb:kb + 128], T.b6[:, 256:384], (), ("RI" + R,), 128, ("b6",))
+            ts(T.VT[:, q4 + 64:q4 + 128], T.RI[:, kb:kb + 64], 63, None, OP.bitwise_and, r=("RI" + R,), w=("VTb" + R,))
+            ts(T.VT[:, q4 + 128:q4 + 192], T.RI[:, kb + 64:kb + 128], 255, None, OP.bitwise_and, r=("RI" + R,), w=("VTa" + R,))
+            mk = ("MKn" + R, "MK0" + R, "MKr" + R, "MKs" + R)
+            mm([(T.b6[:, 0:256], [(T.Ib[:, :], T.MK[:, q4:q4 + 256])])], mk + ("Ib",), (), ("b6",), 256)
+            tt(T.PRD[:, q4:q4 + 256], T.VT[:, q4:q4 + 256], T.b6[:, 0:256], OP.mult, ("VTq" + R, "VTb" + R, "VTa" + R, "VTi" + R), ("PRD" + R,), 256, ("b6",))
+            BA, BB = T.BI[:, 256 * t:256 * t + 128], T.BI[:, 256 * t + 128:256 * t + 256]
+            mm([(T.b6[:, 384:448], [(BA, T.MK[:, q4 + 128:q4 + 192]), (BA, T.MK[:, q4 + 192:q4 + 256]), (BB, T.MK[:, q4 + 64:q4 + 128])]
+                 + [(T.If[:, :], T.PRD[:, q4 + 64 * j:q4 + 64 * j + 64]) for j in range(4)])], mk + ("PRD" + R, "If", "BIa%d" % t, "BIb%d" % t), (), ("b6",), 200)
+            act(Pf, T.b6[:, 384:448], (), ("Pf" + R,), 64, ("b6",))
+            if t < 2:
+                cp(PL, T.b6[:, 384:448], (), ("PL" + R,), 64, ("b6",))
+            else:
+                mm([(T.b6[0:64, 0:128], [(Pf, T.If[:, :])])], ("Pf" + R, "If"), (), ("b6",), 512)
+                act(T.PT[:, r::4], T.b6[0:64, 0:128], (), ("PT" + R,), 128, ("b6",), bias=-16.0)
+        rv = ("RV%d" % t,)
+        mm([(T.b3[:, 64 * k:64 * k + 64], [(T.Ib[:, :], RV[:, :])]) for k in range(8)], rv + ("Ib",), (), ("b3",))
+        for b in (0, 1):
+            tt(T.ler[:, 512 * b:512 * b + 512], T.f0[:, 512 * b:512 * b + 512], T.b3[:, :], OP.is_le, ("f00",), ("ler%d" % b,), 512, ("b3",))
+        cp(T.F[:, B + 256:B + 320], RV[:, :], rv, ("F%d4" % t,), 64, (), 0.5)
+        L4 = key(T.ler[:, :], ("ler0", "ler1"), 4)
+        gather("V", T.Sgs[:, 256:320], T.Sg[:, 0:1024], L4, ("Sg0", "L14"), ("Sgs4",), 64)
+        newsel(4, None, None, T.S[:, B + 256:B + 320], ("T%d4" % t,))
+        fn = tuple("F%d%d" % (t, r) for r in range(5))
+        sn = tuple("T%d%d" % (t, r) for r in range(5))
+        Fr += fn
+        Sr += sn
+        dma("Y", T.yf[:, 320 * t:320 * t + 320], T.F[:, B:B + 320], "doutf", fn)
+        mm([(T.b7[0:8, 0:320], [(T.Ys[:, :], T.S[:, B:B + 320])])], sn + ("Ys",), (), ("b7",), 320)
+        act(T.ysb[:, 320 * t:320 * t + 320], T.b7[0:8, 0:320], (), ("ysb%d" % t,), 320, ("b7",), bias=-16.0)
+        dma("Y", T.ys[:, 320 * t:320 * t + 320], T.ysb[:, 320 * t:320 * t + 320], "douts", ("ysb%d" % t,))
+    for k in range(8):
+        dma("Y", T.yp[16 * k:16 * k + 16, :], T.PT[:, 64 * k:64 * k + 64], "doutp", tuple("PT%d" % r for r in range(4)))
+
+    n = len(ops)
+    succ = [[] for _ in range(n)]
+    for k, o in enumerate(ops):
+        for d in o["h"] | o["s"]: succ[d].append(k)
+    prio = [0.0] * n
+    for k in range(n - 1, -1, -1):
+        o = ops[k]
+        prio[k] = o["d"] + o["b"] + max([prio[s] + 0.08 for s in succ[k]], default=0.0)
+    left = [len(o["h"] | o["s"]) for o in ops]
+    free = {}
+    rdy = {k: 0.0 for k in range(n) if left[k] == 0}
+    order = []
+    while rdy:
+        est = {k: max(rdy[k], free.get(ops[k]["e"], 0.0)) for k in rdy}
+        lo = min(est.values())
+        k = max((k for k in rdy if est[k] <= lo + 0.05), key=lambda k: (prio[k], -k))
+        s = est[k]
+        isd = ops[k]["g"] is not None
+        free[ops[k]["e"]] = s + (0.1 if isd else ops[k]["d"])
+        if ops[k]["e"] == "N": free["N"] = 0.0
+        order.append(k)
+        del rdy[k]
+        for x in succ[k]:
+            left[x] -= 1
+            ops[x]["t"] = max(ops[x].get("t", 0.0), s + ops[k]["d"] + 0.08)
+            if left[x] == 0: rdy[x] = ops[x]["t"]
+    sem = {e: T.sem["s" + e] for e in "VAPG"}
+    queue = {"V": g.vector, "A": g.scalar, "P": g.tensor, "G": g, "Y": g.sync}
+    gtot = {}
+    for o in ops:
+        if o["g"] and o["g"] != "send": gtot[o["g"]] = gtot.get(o["g"], 0) + 16
+    cnt = {e: 0 for e in "VAPG"}
+    done = {}
+    seen = {e: {} for e in ENG}
+    know = {}
+    for k in order:
+        o = ops[k]
+        e = o["e"]
+        need = {}
+        for d in o["h"] | o["s"]:
+            if d in o["s"] and ops[d]["e"] == e and o["g"] is None and ops[d]["g"] is None: continue
+            if e == "N": continue
+            for kk, v in (done[d],):
+                if kk is not None: need[kk] = max(need.get(kk, 0), v)
+        if e == "N":
+            done[k] = (o["f"][0], o["f"][1])
+            know[k] = {}
+            continue
+        hit = {}
+        for kk in need:
+            if seen[e].get(kk, 0) < need[kk]: hit[kk] = need[kk]
+        for d in o["h"] | o["s"]:
+            if done[d][0] in hit and done[d][1] <= hit[done[d][0]]:
+                for kk, v in know[d].items():
+                    if kk in hit and kk != done[d][0] and v >= hit[kk]: del hit[kk]
+        for kk, v in hit.items():
+            queue[e].wait_ge(T.sem[kk], int(v))
+            seen[e][kk] = v
+        for d in o["h"] | o["s"]:
+            if d in o["s"] and ops[d]["e"] == e: continue
+            for kk, v in know[d].items(): seen[e][kk] = max(seen[e].get(kk, 0), v)
+        if o["g"] is not None:
+            o["f"](None)
+            done[k] = (None, 0) if o["g"] == "send" else (o["g"], gtot[o["g"]])
+            know[k] = dict(seen[e])
+        else:
+            def inc(i, e=e):
+                cnt[e] += 1
+                i.then_inc(sem[e], 1)
+            o["f"](inc)
+            done[k] = ("s" + e, cnt[e])
+            know[k] = dict(seen[e])
+            know[k]["s" + e] = cnt[e]
+    for e in "VAPG": g.wait_ge(sem[e], cnt[e])
+    for q in gtot: g.wait_ge(T.sem[q], gtot[q])
+    nl = 0
+    for t in range(3):
+        nl += len(topo.engines(core, T.cores[(rank + 1 + t % 3) % 4])[:8])
+        g.wait_ge(T.sem["rv%d" % t], len(topo.engines(T.cores[(rank - 1 - t % 3) % 4], core)[:8]))
+    g.wait_ge(T.sem["ls"], nl)

@@ -7,7 +7,7 @@ AF = ActivationFunctionType
 SCRATCH = {}
 for _n, _c, _d in (
         ("F", 4112, "bfloat16"), ("S", 4112, "bfloat16"), ("SELw", 3152, "bfloat16"), ("C1", 3152, "bfloat16"), ("C2", 3152, "bfloat16"),
-        ("f0", 4096, "bfloat16"), ("f1", 4096, "bfloat16"), ("Sg", 4096, "bfloat16"), ("le", 16384, "bfloat16"), ("ler", 1024, "bfloat16"),
+        ("f0", 4096, "bfloat16"), ("f1", 12288, "bfloat16"), ("Sg", 4096, "bfloat16"), ("le", 16384, "bfloat16"), ("ler", 1024, "bfloat16"),
         ("Gb", 256, "bfloat16"), ("Gr", 2048, "bfloat16"), ("Sgs", 320, "bfloat16"), ("QL", 768, "uint16"), ("Rl", 1024, "float32"),
         ("X", 1024, "float32"), ("X2", 512, "float32"), ("X3", 256, "float32"), ("XI", 256, "int32"), ("CI", 256, "int32"),
         ("cb", 256, "bfloat16"), ("VT", 1024, "int32"), ("MK", 1024, "bfloat16"), ("PRD", 1024, "float32"), ("RI", 512, "int32"),
@@ -21,8 +21,7 @@ for _n, _c, _d in (
         ("BI", 768, "bfloat16"), ("Z0", 144, "bfloat16"), ("Z1", 144, "bfloat16"), ("Z2", 144, "bfloat16"), ("Z3", 144, "bfloat16"),
         ("K63", 64, "bfloat16"), ("Zh", 144, "bfloat16"), ("C512", 64, "bfloat16"), ("half", 1, "float32"), ("OFF", 192, "bfloat16"), ("ki", 768, "int32"), ("ki2", 768, "int32"), ("ki3", 768, "int32"), ("KB", 512, "bfloat16"),
         ("gi", 384, "int32"), ("gi2", 384, "int32"), ("GM", 384, "bfloat16"), ("Ys", 8, "bfloat16"),
-        ("T1", 512, "bfloat16"), ("T2", 512, "bfloat16"), ("T3", 512, "bfloat16"), ("T4", 512, "bfloat16"), ("XT", 512, "bfloat16"),
-        ("bi", 16, "float32"), ("bc", 16, "float32")):
+        ("vh", 256, "float32"), ("VH", 256, "bfloat16"), ("VL", 256, "bfloat16")):
     SCRATCH[_n] = ("sbuf", [128, _c], _d)
 SCRATCH["PS"] = ("sbuf", [64, 512], "int32")
 SCRATCH["PSf"] = ("sbuf", [64, 512], "float32")
@@ -36,12 +35,50 @@ SCRATCH["SSf"] = ("sbuf", [49, 512], "float32")
 SCRATCH["ysb"] = ("sbuf", [8, 960], "float32")
 for _k in range(8):
     SCRATCH["b%d" % _k] = ("psum", [128, 512], "float32")
-GROUPS = ["dpar", "dsel", "dsl", "dfr", "dsw", "ds1", "ds2", "ds3", "doutf", "douts", "doutp"]
+GROUPS = ["dpar", "dsel", "dsl", "dfr", "dsw", "ds0", "ds1", "ds2", "ds3", "doutf", "douts", "doutp"]
 SEMAPHORES = ["sV", "sA", "sP", "sG", "rv0", "rv1", "rv2", "ls"] + GROUPS
 ENG = ("V", "A", "P", "G", "Y")
-SIGN = (0, 1)
-GAM = 1.56
-CY = 0.00104
+MODES = ("CSFF", "SFFF", "SCFF", "CSSF")
+CY = 0.00095
+MODEL = {"cy": 0.00095, "gam": 1.56, "pe": 0.00045, "sem": 0.07, "eps": 0.05, "chunk": 0.0, "vb": 1.0}
+NOISE = None
+
+
+def schedule(ops, succ, M, noise=None):
+    n = len(ops)
+    d = [o["c"][0] + M["cy"] * (o["c"][1] + o["c"][2] * M["gam"]) + o["c"][3] * M["pe"] for o in ops]
+    prio = [0.0] * n
+    for k in range(n - 1, -1, -1):
+        m = 0.0
+        for s in succ[k]:
+            if prio[s] > m: m = prio[s]
+        prio[k] = d[k] + M["sem"] + ops[k]["b"] - M["chunk"] * (ops[k]["m"] % 10 in (1, 2, 3)) + m + (noise[k % len(noise)] if noise else 0.0)
+    left = [len(o["h"] | o["s"]) for o in ops]
+    at = [0.0] * n
+    free = {e: 0.0 for e in "VAPGYN"}
+    where = [o["e"] for o in ops]
+    rdy = [k for k in range(n) if left[k] == 0]
+    order, end = [], 0.0
+    while rdy:
+        lo = 1e9
+        est = []
+        for k in rdy:
+            e = where[k]
+            if e == "*": e = "V" if max(at[k], free["V"]) + M["vb"] < max(at[k], free["A"]) else "A"
+            s = max(at[k], free[e])
+            est.append((k, e, s))
+            if s < lo: lo = s
+        k, e, s = max((x for x in est if x[2] <= lo + M["eps"]), key=lambda x: (prio[x[0]], -x[0]))
+        where[k] = e
+        if e != "N": free[e] = s + (0.1 if ops[k]["g"] is not None else d[k])
+        order.append(k)
+        rdy.remove(k)
+        end = max(end, s + d[k])
+        for x in succ[k]:
+            left[x] -= 1
+            at[x] = max(at[x], s + d[k] + M["sem"])
+            if left[x] == 0: rdy.append(x)
+    return order, where, end
 
 
 def rank_program(g, core, T, topo):
@@ -49,7 +86,7 @@ def rank_program(g, core, T, topo):
     if rank is None:
         return
     ops = []
-    early = [0.0]
+    early, mark = [0.0], [0]
     lastw, readers, psum = {}, {}, {}
 
     def op(eng, fn, r=(), w=(), d=0.1, ps=(), grp=None, bias=0.0):
@@ -64,22 +101,24 @@ def rank_program(g, core, T, topo):
         for x in w: lastw[x] = k; readers[x] = set()
         for b in ps:
             runs = psum.setdefault(b, [])
-            if not runs or runs[-1][0] != eng: runs.append((eng, []))
+            if not runs or runs[-1][0] != eng or eng == "*": runs.append((eng, []))
             runs[-1][1].append(k)
             if len(runs) > 1: hard |= set(runs[-2][1])
         hard.discard(k); soft.discard(k)
-        ops.append({"e": eng, "f": fn, "h": hard, "s": soft - hard, "d": d, "g": grp, "b": bias + early[0]})
+        ops.append({"e": eng, "f": fn, "h": hard, "s": soft - hard, "c": d if isinstance(d, tuple) else (d, 0, 0, 0), "g": grp, "b": bias + early[0], "m": mark[0], "any": eng == "*"})
         return k
 
     V, A, TE = g.vector, g.scalar, g.tensor
 
-    def vd(n, c=1.0): return max(64, n * c) * CY + 0.03
-    def gd(n): return 0.06 + n * GAM * CY
-    def ad(n): return max(64, n) * CY + 0.06
+    def vd(n, c=1.0): return (0.02, max(64, n * c), 0, 0)
+    def gd(n): return (0.06, 0, n, 0)
+    def ad(n): return (0.04, max(64, n), 0, 0)
 
-    def gather(eng, out, win, off, r, w, n):
-        if eng == "V": op("V", lambda inc: inc(V.tensor_copy(out, win.indirect(off))), r, w, gd(n))
-        else: op("A", lambda inc: inc(A.activation(out, win.indirect(off), AF.Copy)), r, w, gd(n))
+    def gather(out, win, off, r, w, n):
+        op("*", lambda inc, e: inc(V.tensor_copy(out, win.indirect(off)) if e == "V" else A.activation(out, win.indirect(off), AF.Copy)), r, w, gd(n))
+
+    def mv(out, i0, r=(), w=(), n=64, ps=(), h=1.0):
+        op("*", lambda inc, e: inc(V.tensor_copy(out, i0) if e == "V" else A.activation(out, i0, AF.Copy)), r, w, ad(n), ps)
 
     def ts(out, i0, s1, s2, o1, o2=None, r=(), w=(), n=64, ps=(), c=1.0):
         if o2 is None: op("V", lambda inc: inc(V.tensor_scalar(out, i0, s1, None, o1)), r, w, vd(n, c), ps)
@@ -100,11 +139,11 @@ def rank_program(g, core, T, topo):
                 for j, (a, b) in enumerate(prs):
                     z = TE.matmul(out, a, b, j == 0, j == len(prs) - 1)
                 inc(z)
-        op("P", fn, r, w, sum(len(p) for _, p in groups) * max(64, n) * 0.0006 + 0.1, ps)
+        op("P", fn, r, w, (0.06, 0, 0, sum(len(p) for _, p in groups) * max(64, n)), ps)
 
-    def dma(eng, out, in_, grp, r=(), w=(), d=2.0):
+    def dma(eng, out, in_, grp, r=(), w=(), d=2.0, bias=0.0):
         q = {"Y": g.sync, "A": g.scalar}[eng]
-        op(eng, lambda inc: q.dma_start(out, in_).then_inc(T.sem[grp], 16), r, w, d, grp=grp)
+        op(eng, lambda inc: q.dma_start(out, in_).then_inc(T.sem[grp], 16), r, w, d, grp=grp, bias=bias)
 
     def iota(out, pat, base, cm, w, n, flag=True):
         if flag: op("G", lambda inc: inc(g.iota(out, pat, base, cm, allow_small_or_imprecise_dtypes=True)), (), w, 0.13 + 2 * n * CY)
@@ -113,19 +152,18 @@ def rank_program(g, core, T, topo):
     def fill(ap, c, w, n): op("V", lambda inc: inc(V.memset(ap, c)), (), w, vd(n, 0.5))
 
     B0 = 3152
-    dma("Y", T.sl[:, :], T.sel0[:, :], "dsl", (), ("sl",))
+    dma("Y", T.sl[:, :], T.sel0[:, :], "dsl", (), ("sl",), bias=50.0)
+    dma("Y", T.F[:, 16:B0], T.front[:, :], "dfr", (), ("Fi",), 6.0, 30.0)
     for k in range(8):
         dma("A" if k % 2 else "Y", T.PS[:, 64 * k:64 * k + 64], T.par[16 * k:16 * k + 16, :], "dpar", (), ("PS%d" % k,))
     for k in range(8):
         dma("A" if k % 2 else "Y", T.SS[:, 64 * k:64 * k + 64], T.sel0[k:k + 1, :], "dsel", (), ("SS%d" % k,))
-    dma("Y", T.F[:, 16:B0], T.front[:, :], "dfr", (), ("Fi",), 6.0)
     iota(T.pi[:, :], [[0, 1]], 0, 1, ("pi",), 1, False)
     iota(T.iu[:, :], [[1, 144]], 0, 0, ("iu",), 144)
     iota(T.ib[:, :], [[0, 8], [1, 16]], 0, 0, ("ib",), 128)
     iota(T.irk[:, :], [[0, 16], [1, 4]], 0, 0, ("irk",), 64)
-    iota(T.bi[:, :], [[512, 16]], 0, 0, ("bi",), 16)
-    iota(T.T1[:, :], [[16, 32], [0, 16]], 0, 0, ("T1",), 512)
-    iota(T.T2[:, :], [[0, 32], [1, 16]], 0, 0, ("T2",), 512)
+    iota(T.vh[:, :], [[16, 16], [0, 16]], 16, 0, ("vh",), 256)
+    iota(T.VL[:, :], [[0, 16], [1, 16]], 0, 0, ("VL",), 256)
     iota(T.K63[:, :], [[-1, 64]], 63, 0, ("K63",), 64)
     iota(T.i16[:, :], [[16, 8]], 15, 0, ("i16",), 8)
     iota(T.ki[:, 0:256], [[1, 4], [1, 16], [64, 4]], 0, 0, ("ki0",), 256, False)
@@ -134,6 +172,10 @@ def rank_program(g, core, T, topo):
     iota(T.gi[:, :], [[1, 6], [0, 16], [4, 4]], 0, 0, ("gi",), 384, False)
     fill(T.F[:, 0:16], 0.0, ("Fz",), 16)
     fill(T.SELw[:, :], 0.0, ("SELw",), 3152)
+    early[0] = -6.0
+    for k in range(8): fill(T.S[:, 514 * k:514 * k + 514], 0.0, ("Sz%d" % k,), 514)
+    early[0] = 0.0
+    Sz = tuple("Sz%d" % k for k in range(8))
     fill(T.C1[:, 0:16], 0.0, ("C1z",), 16)
     for k in range(3): fill(T.OFF[:, 64 * k:64 * k + 64], 8192.0 * (k + 1), ("OFF%d" % k,), 64)
     ts(T.pii[:, 0:1], T.pi[:, :], 15, None, OP.bitwise_and, r=("pi",), w=("pii0",))
@@ -146,7 +188,7 @@ def rank_program(g, core, T, topo):
     ts(T.pc[:, 3:4], T.pc[:, 1:2], 1008.0, None, OP.add, r=("pc1",), w=("pc3",))
     cp(T.pc[:, 4:5], T.pii[:, 1:2], ("pii1",), ("pc4",))
     for k in (1, 2, 3): ts(T.pc[:, 4 + k:5 + k], T.pc[:, 4:5], float(k), None, OP.is_equal, r=("pc4",), w=("pc%d" % (4 + k),))
-    for k in (0, 1): ts(T.pc[:, 8 + k:9 + k], T.pc[:, 1:2], float(k), None, OP.is_equal, r=("pc1",), w=("pc%d" % (8 + k),))
+    ts(T.pc[:, 8:9], T.pc[:, 1:2], 256.0, None, OP.mult, r=("pc1",), w=("pc8",))
     ts(T.pc[:, 10:11], T.pc[:, 4:5], 3.0, None, OP.is_lt, r=("pc4",), w=("pc10",))
     cp(T.pc[:, 11:12], T.pii[:, 2:3], ("pii2",), ("pc11",))
     ts(T.pc[:, 12:13], T.pc[:, 1:2], 20.0, None, OP.mult, r=("pc1",), w=("pc12",))
@@ -178,16 +220,10 @@ def rank_program(g, core, T, topo):
         ts(T.VT[:, 256 * r + 192:256 * r + 256], T.ki[:, 512 + 64 * r:576 + 64 * r], T.pc[:, 13:14], None, OP.add, r=("ki2", "pc13"), w=("VTi%d" % r,))
     ts(T.gi2[:, :], T.gi[:, :], 15, None, OP.bitwise_and, r=("gi",), w=("gi2",), n=384)
     ts(T.GM[:, :], T.gi2[:, :], T.pc[:, 1:2], None, OP.is_equal, r=("gi2", "pc1"), w=("GM",), n=384)
-    early[0] = 30.0
-    ts(T.T3[:, :], T.T1[:, :], T.pc[:, 8:9], None, OP.mult, r=("T1", "pc8"), w=("T3",), n=512, c=0.5)
-    ts(T.T4[:, :], T.T2[:, :], T.pc[:, 9:10], None, OP.mult, r=("T2", "pc9"), w=("T4",), n=512, c=0.5)
-    tt(T.XT[:, :], T.T3[:, :], T.T4[:, :], OP.add, ("T3", "T4"), ("XT",), 512)
-    ts(T.bc[:, :], T.bi[:, :], T.pc[:, 8:9], None, OP.mult, r=("bi", "pc8"), w=("bc",))
-    for k in range(9):
-        e = min(4112, 512 * k + 512)
-        act(T.S[:, 512 * k:e], T.XT[:, 0:e - 512 * k], ("XT", "bc"), ("Sv%d" % k,), 512, f=AF.Identity, bias=T.bc[:, k:k + 1])
-    Sv = tuple("Sv%d" % k for k in range(9))
-    early[0] = 0.0
+    op("A", lambda inc: inc(A.activation(T.VH[:, :], T.vh[:, :], AF.Identity, bias=T.pc[:, 8:9])), ("vh", "pc8"), ("VH",), ad(256))
+    dma("Y", T.S[0::16, 16:4112], T.VH[:, :], "ds0", ("VH",) + Sz, ("S0",))
+    dma("Y", T.S[1::16, 16:4112], T.VL[:, :], "ds0", ("VL",) + Sz, ("S1",))
+    Sv = Sz
     ts(T.PSf[:, :], T.PS[:, :], 16.0, None, OP.add, r=tuple("PS%d" % k for k in range(8)), w=("PSf",), n=512)
     mm([(T.b6[:, 64 * r:64 * r + 64], [(T.PSf[:, r::4], T.If[0:64, 0:64])]) for r in range(4)], ("PSf", "If"), (), ("b6",), 256)
     cp(T.PL[:, :], T.b6[:, 0:256], (), tuple("PL%d" % r for r in range(4)), 256, ("b6",))
@@ -201,10 +237,10 @@ def rank_program(g, core, T, topo):
     dma("Y", T.SELw[2::16, 16:B0], T.slh[:, :], "dsw", ("slh", "SELw"), ("SW2",))
     dma("Y", T.SELw[3::16, 16:B0], T.sll[:, :], "dsw", ("sll", "SELw"), ("SW3",))
     for r in range(4):
-        gather("VA"[r % 2], T.C1[:, 16 + r:B0:4], T.SELw[:, :], T.LS[:, 50 * r:50 * r + 49], ("SELw", "SW2", "SW3", "LS%d" % r), ("C1%d" % r,), 784)
+        gather(T.C1[:, 16 + r:B0:4], T.SELw[:, :], T.LS[:, 50 * r:50 * r + 49], ("SELw", "SW2", "SW3", "LS%d" % r), ("C1%d" % r,), 784)
     c1 = ("C1z",) + tuple("C1%d" % r for r in range(4))
     for r in range(4):
-        gather("VA"[r % 2], T.C2[:, 16 + r:B0:4], T.C1[:, :], T.LS[:, 50 * r:50 * r + 49], c1 + ("LS%d" % r,), ("C2%d" % r,), 784)
+        gather(T.C2[:, 16 + r:B0:4], T.C1[:, :], T.LS[:, 50 * r:50 * r + 49], c1 + ("LS%d" % r,), ("C2%d" % r,), 784)
     c2 = tuple("C2%d" % r for r in range(4))
     for k in (0, 1):
         dma("Y", T.S[2 + k::16, 16:B0], T.SELw[2 + k::16, 16:B0], "ds1", ("SW2", "SW3") + Sv, ("S%d" % (2 + k),))
@@ -212,7 +248,8 @@ def rank_program(g, core, T, topo):
         dma("Y", T.S[4 + k::16, 16:B0], T.C1[2 + k::16, 16:B0], "ds2", c1 + Sv, ("S%d" % (4 + k),))
     for k in (0, 1):
         dma("Y", T.S[6 + k::16, 16:B0], T.C2[2 + k::16, 16:B0], "ds3", c2 + Sv, ("S%d" % (6 + k),))
-    Sr = Sv + tuple("S%d" % k for k in range(2, 8))
+    Sr = Sv + tuple("S%d" % k for k in range(8))
+    Sv = Sz + ("S0", "S1")
     Fr = ("Fi", "Fz")
 
     def z(n, y): return T["Z%s" % n][:, 15 - y:143 - y]
@@ -227,7 +264,7 @@ def rank_program(g, core, T, topo):
 
     def newsel(n, r, sv, cols, w):
         mm([(T.b7[:, 0:64], [(T.Sh[:, :], T.Sgs[:, 64 * n:64 * n + 64]), (T.Ib[:, :], cols)])], ("Sgs%d" % n, "Sh", "Ib") + Sv, (), ("b7",))
-        act(cols, T.b7[:, 0:64], (), w, 64, ("b7",))
+        mv(cols, T.b7[:, 0:64], (), w, 64, ("b7",))
 
     for t in range(3):
         B = B0 + 320 * t
@@ -240,40 +277,52 @@ def rank_program(g, core, T, topo):
             R = "%d" % r
             PL, Pf = T.PL[:, q0:q0 + 64], T.Pf[:, q0:q0 + 64]
             f0, f1, Sg = T.f0[:, 1024 * r:1024 * r + 1024], T.f1[:, 1024 * r:1024 * r + 1024], T.Sg[:, 1024 * r:1024 * r + 1024]
-            gather("A", f0, win, PL, Fr + ("PL" + R,), ("f0" + R,), 1024)
-            gather("A", Sg, swin, PL, Sr + ("PL" + R,), ("Sg" + R,), 1024)
-            L1 = key(f0, ("f0" + R,), r)
-            gather("V", T.Gb[:, q0:q0 + 64], f0, L1, ("f0" + R, "L1" + R), ("Gb" + R,), 64)
-            mm([(GP[:, 64 * k:64 * k + 64], [(T.Ib[:, :], T.Gb[:, q0:q0 + 64])]) for k in range(8)], ("Gb" + R, "Ib"), (), (GPb,))
-            act(T.Gr[:, 512 * r:512 * r + 512], GP[:, :], (), ("Gr" + R,), 512, (GPb,))
-            grp = [(Q[:, 0:64], [(T.If[:, :], Pf)])]
+            mark[0] = 10 * t + r
+            for b in (0, 1):
+                gather(f0[:, 512 * b:512 * b + 512], win, PL[:, 32 * b:32 * b + 32], Fr + ("PL" + R,), ("f0%d%d" % (r, b),), 512)
+            for b in (0, 1):
+                gather(Sg[:, 512 * b:512 * b + 512], swin, PL[:, 32 * b:32 * b + 32], Sr + ("PL" + R,), ("Sg%d%d" % (r, b),), 512)
+            f0k, Sgk = ("f0%d0" % r, "f0%d1" % r), ("Sg%d0" % r, "Sg%d1" % r)
+            L1 = key(f0, f0k, r)
+            gather(T.Gb[:, q0:q0 + 64], f0, L1, f0k + ("L1" + R,), ("Gb" + R,), 64)
+            g5 = 512 * r
+            mv(T.Gr[:, g5:g5 + 64], T.Gb[:, q0:q0 + 64], ("Gb" + R,), ("Gra" + R,), 64)
+            mv(T.Gr[:, g5 + 64:g5 + 128], T.Gb[:, q0:q0 + 64], ("Gb" + R,), ("Grb" + R,), 64)
+            mv(T.Gr[:, g5 + 128:g5 + 256], T.Gr[:, g5:g5 + 128], ("Gra" + R, "Grb" + R), ("Grc" + R,), 128)
+            mv(T.Gr[:, g5 + 256:g5 + 512], T.Gr[:, g5:g5 + 256], ("Gra" + R, "Grb" + R, "Grc" + R), ("Grd" + R,), 256)
+            Gk = tuple("Gr%s%d" % (x, r) for x in "abcd")
+            MD = MODES[r]
+            mm([(Q[:, 0:64], [(T.If[:, :], Pf)])], ("Pf" + R, "If"), (), (Qb,), 256)
             for h in (1, 2, 3):
-                grp.append((Q[:, 64 * h:64 * h + 64], [(z(h, y), Sg[:, y::16]) for y in range(16)] + [(T.Ib[:, :], T.OFF[:, 64 * h - 64:64 * h])]))
-            mm(grp, ("Pf" + R, "If", "Sg" + R, "Z1", "Z2", "Z3", "Ib", "OFF0", "OFF1", "OFF2"), (), (Qb,))
+                mm([(Q[:, 64 * h:64 * h + 64], [(z(h, y), Sg[:, y::16]) for y in range(16)] + [(T.Ib[:, :], T.OFF[:, 64 * h - 64:64 * h])])],
+                   Sgk + ("Z%d" % h, "Ib", "OFF%d" % (h - 1)), (), (Qb,))
             for h in (1, 2, 3):
                 a = 192 * r + 64 * h - 64
                 ts(T.QL[:, a:a + 64], Q[:, 64 * h:64 * h + 64], -8192.0 * h, None, OP.add, w=("QL%d%d" % (r, h),), ps=(Qb,))
-            gather("A", f1, win, T.QL[:, 192 * r:192 * r + 64], Fr + ("QL%d1" % r,), ("f1" + R,), 1024)
-            gather("V", T.Sgs[:, q0:q0 + 64], Sg, L1, ("Sg" + R, "L1" + R), ("Sgs" + R,), 64)
+            fh = [f0] + [T.f1[:, 4096 * (h - 1) + 1024 * r:4096 * (h - 1) + 1024 * r + 1024] for h in (1, 2, 3)]
+            for h in (1, 2, 3):
+                for b in (0, 1):
+                    a = 192 * r + 64 * h - 64 + 32 * b
+                    if MD[h] != "F": gather(fh[h][:, 512 * b:512 * b + 512], win, T.QL[:, a:a + 32], Fr + ("QL%d%d" % (r, h),), ("f%d%d%d" % (h, r, b),), 512)
+            gather(T.Sgs[:, q0:q0 + 64], Sg, L1, Sgk + ("L1" + R,), ("Sgs" + R,), 64)
             for h in range(4):
+                if MD[h] == "C": mm([(GP[:, :], [(T.Ib[:, :], T.Gr[:, g5:g5 + 512])])], Gk + ("Ib",), (), (GPb,), 512)
                 for b in (0, 1):
                     le = T.le[:, 4096 * r + 1024 * h + 512 * b:4096 * r + 1024 * h + 512 * b + 512]
                     k = ("le%d%d%d" % (r, h, b),)
-                    if h in SIGN:
+                    if MD[h] == "S":
                         D, Db = T["b%d" % (3 + b)], "b%d" % (3 + b)
-                        mm([(D[:, :], [(T.In[:, :], (f0, f1)[h][:, 512 * b:512 * b + 512]), (T.Ib[:, :], T.Gr[:, 512 * r:512 * r + 512])])],
-                           ("f%d" % h + R, "Gr" + R, "In", "Ib"), (), (Db,), 512)
+                        mm([(D[:, :], [(T.In[:, :], fh[h][:, 512 * b:512 * b + 512]), (T.Ib[:, :], T.Gr[:, 512 * r:512 * r + 512])])],
+                           ("f%d%d%d" % (h, r, b), "In", "Ib") + Gk, (), (Db,), 512)
                         op("A", lambda inc, le=le, D=D: inc(A.activation(le, D[:, :], AF.Sign, bias=T.half[:, :])), ("half",), k, ad(512), (Db,))
-                    elif h < 2:
-                        tt(le, (f0, f1)[h][:, 512 * b:512 * b + 512], GP[:, :], OP.is_le, ("f%d" % h + R,), k, 512, (GPb,))
+                    elif MD[h] == "C":
+                        tt(le, fh[h][:, 512 * b:512 * b + 512], GP[:, :], OP.is_le, ("f%d%d%d" % (h, r, b),), k, 512, (GPb,))
                     else:
                         a = 192 * r + 64 * h - 64 + 32 * b
                         op("V", lambda inc, le=le, a=a, r=r, win=win: inc(V.tensor_tensor(le, win.indirect(T.QL[:, a:a + 32]), T.Gr[:, 512 * r:512 * r + 512], OP.is_le)),
-                           Fr + ("QL%d%d" % (r, h), "Gr" + R), k, gd(512))
-                lh = 4096 * r + 1024 * h
-                sg = h in SIGN
-                mm([(T.b5[:, 64 * h:64 * h + 64], [(z("h" if sg else 0, y), T.le[:, lh + y:lh + 1024:16]) for y in range(16)] + ([(T.Ib[:, :], T.C512[:, :])] if sg else []))],
-                   ("le%d%d0" % (r, h), "le%d%d1" % (r, h), "Z0", "Zh", "C512", "Ib"), (), ("b5",))
+                           Fr + Gk + ("QL%d%d" % (r, h),), k, gd(512))
+                lh, sg = 4096 * r + 1024 * h, MD[h] == "S"
+                mm([(T.b5[:, 64 * h:64 * h + 64], [(z("h" if sg else 0, y), T.le[:, lh + y:lh + 1024:16]) for y in range(16)] + ([(T.Ib[:, :], T.C512[:, :])] if sg else []))], ("le%d%d0" % (r, h), "le%d%d1" % (r, h), "Z0", "Zh", "C512", "Ib"), (), ("b5",))
             act(T.Rl[:, q4:q4 + 256], T.b5[:, 0:256], (), ("Rl" + R,), 256, ("b5",), AF.Relu, 786432.0, -1024.0)
             tt(Q[:, 256:384], T.Rl[:, q4 + 128:q4 + 256], Q[:, 128:256], OP.add, ("Rl" + R,), ("XP" + Qb,), 128, (Qb,))
             tt(T.X[:, q4:q4 + 128], T.Rl[:, q4:q4 + 128], Q[:, 0:128], OP.add, ("Rl" + R,), ("X" + R,), 128, (Qb,))
@@ -284,16 +333,19 @@ def rank_program(g, core, T, topo):
             ts(T.VT[:, q4:q4 + 64], T.XI[:, q0:q0 + 64], 8191, None, OP.bitwise_and, r=("XI" + R,), w=("VTq" + R,))
             cp(T.QE[:, q0:q0 + 64], T.VT[:, q4:q4 + 64], ("VTq" + R,), ("QE" + R,))
             h5 = 512 * r
-            gather("A", T.H[:, h5:h5 + 512], win, T.QE[:, q0 + 32:q0 + 64], Fr + ("QE" + R,), ("H" + R,), 512)
-            op("V", lambda inc, h5=h5, q0=q0, win=win: inc(V.tensor_tensor(T.AC[:, h5:h5 + 512], win.indirect(T.QE[:, q0:q0 + 32]), T.H[:, h5:h5 + 512], OP.max)),
-               Fr + ("QE" + R, "H" + R), ("AC" + R,), gd(512))
-            tt(T.b7[:, 384:512], T.AC[:, h5 + 128:h5 + 256], T.AC[:, h5 + 384:h5 + 512], OP.max, ("AC" + R,), ("AP",), 256, ("b7",))
-            tt(T.A2[:, q4:q4 + 128], T.AC[:, h5:h5 + 128], T.AC[:, h5 + 256:h5 + 384], OP.max, ("AC" + R,), ("A2" + R,), 128)
-            tt(T.b7[:, 320:384], T.A2[:, q4 + 64:q4 + 128], T.b7[:, 448:512], OP.max, ("A2" + R, "AP"), ("AQ",), 64, ("b7",))
-            tt(T.A3[:, 128 * r:128 * r + 64], T.A2[:, q4:q4 + 64], T.b7[:, 384:448], OP.max, ("A2" + R, "AP"), ("A3" + R,), 64, ("b7",))
-            tt(T.A4[:, q0:q0 + 64], T.A3[:, 128 * r:128 * r + 64], T.b7[:, 320:384], OP.max, ("A3" + R, "AQ"), ("A4" + R,), 64, ("b7",))
+            for b in (1, 0):
+                hb = h5 + 256 * b
+                gather(T.H[:, hb:hb + 256], win, T.QE[:, q0 + 32 + 16 * b:q0 + 48 + 16 * b], Fr + ("QE" + R,), ("H%d%d" % (r, b),), 256)
+                op("V", lambda inc, hb=hb, a=q0 + 16 * b, win=win: inc(V.tensor_tensor(T.AC[:, hb:hb + 256], win.indirect(T.QE[:, a:a + 16]), T.H[:, hb:hb + 256], OP.max)),
+                   Fr + ("QE" + R, "H%d%d" % (r, b)), ("AC%d%d" % (r, b),), gd(256))
+                if b: mm([(T.b7[:, 256:512], [(T.Ib[:, :], T.AC[:, hb:hb + 256])])], ("AC%d1" % r, "Ib"), (), ("b7",), 256)
+            tt(T.b7[:, 128:256], T.AC[:, h5 + 128:h5 + 256], T.b7[:, 384:512], OP.max, ("AC%d0" % r,), ("AP",), 128, ("b7",))
+            tt(T.A2[:, q4:q4 + 128], T.AC[:, h5:h5 + 128], T.b7[:, 256:384], OP.max, ("AC%d0" % r,), ("A2" + R,), 128, ("b7",))
+            tt(T.b7[:, 64:128], T.A2[:, q4 + 64:q4 + 128], T.b7[:, 192:256], OP.max, ("A2" + R, "AP"), ("AQ",), 64, ("b7",))
+            tt(T.A3[:, 128 * r:128 * r + 64], T.A2[:, q4:q4 + 64], T.b7[:, 128:192], OP.max, ("A2" + R, "AP"), ("A3" + R,), 64, ("b7",))
+            tt(T.b7[:, 0:64], T.A3[:, 128 * r:128 * r + 64], T.b7[:, 64:128], OP.max, ("A3" + R, "AQ"), ("A4",), 64, ("b7",))
             gm = 64 * (r + t)
-            tt(T.A5[:, q0:q0 + 64], T.A4[:, q0:q0 + 64], T.GM[:, gm:gm + 64], OP.add, ("A4" + R, "GM"), ("A5" + R,), 64)
+            tt(T.A5[:, q0:q0 + 64], T.GM[:, gm:gm + 64], T.b7[:, 0:64], OP.add, ("A4", "GM"), ("A5" + R,), 64, ("b7",))
             fk = "F%d%d" % (t, r)
             if r == 0:
                 NF, RV = T["NF%d" % t], T["RV%d" % t]
@@ -308,14 +360,14 @@ def rank_program(g, core, T, topo):
                     g.remote_dma(RV[:, :], NF[:, :], T.sem["rv%d" % t], T.sem["ls"], pid, rid, sum(1 << e for e in ne))
                 op("G", send, ("NF%d" % t,), ("sent%d" % t,), 1.5, grp="send")
                 op("N", ("rv%d" % t, nr), ("sent%d" % t,), ("RV%d" % t,), 2.5)
-                act(T.F[:, B + r:B + 256:4], NF[:, :], ("NF%d" % t,), (fk,), 64)
+                mv(T.F[:, B + r:B + 256:4], NF[:, :], ("NF%d" % t,), (fk,), 64)
             else:
                 ts(T.F[:, B + r:B + 256:4], T.A5[:, q0:q0 + 64], 255.0, None, OP.min, r=("A5" + R,), w=(fk,), c=0.5)
             newsel(r, r, None, T.S[:, B + r:B + 256:4], ("T%d%d" % (t, r),))
             m4 = 8 * r
             cp(T.mb[:, m4:m4 + 4], T.mi[:, m4:m4 + 4], ("mi" + R,), ("mb" + R,))
             mm([(T.b6[0:4, 256:384], [(T.mb[:, m4:m4 + 4], T.Ib[:, :])])], ("mb" + R, "Ib"), (), ("b6",), 128)
-            act(T.mT[:, 128 * r:128 * r + 128], T.b6[0:4, 256:384], (), ("mT" + R,), 128, ("b6",))
+            mv(T.mT[:, 128 * r:128 * r + 128], T.b6[0:4, 256:384], (), ("mT" + R,), 128, ("b6",))
             mm([(T.b6[:, 0:64], [(T.mT[:, 128 * r:128 * r + 128], T.Rk[0:4, :]), (T.In[:, :], T.K63[:, :])])], ("mT" + R, "Rk", "In", "K63"), (), ("b6",))
             ts(T.MK[:, q4 + 192:q4 + 256], T.b6[:, 0:64], 0.0, None, OP.is_equal, w=("MKs" + R,), ps=("b6",))
             ts(T.MK[:, q4:q4 + 64], T.X3[:, q0:q0 + 64], 8192.0, None, OP.is_ge, r=("X3" + R,), w=("MKn" + R,))
@@ -325,7 +377,7 @@ def rank_program(g, core, T, topo):
             tt(T.MK[:, q4 + 64:q4 + 128], T.MK[:, q4:q4 + 64], T.MK[:, q4 + 192:q4 + 256], OP.is_equal, ("MKn" + R, "MKs" + R), ("MK0" + R,), 64)
             red, cb = T.MK[:, q4 + 128:q4 + 192], T.cb[:, q0:q0 + 64]
             mm([(T.b6[0:64, 0:128], [(red, T.GA[:, :])]), (T.b6[0:64, 128:256], [(red, T.GA[:, :]), (cb, T.Ib[:, :])])], ("MKr" + R, "cb" + R, "GA", "Ib"), (), ("b6",), 128)
-            act(T.FT[:, q4:q4 + 256], T.b6[0:64, 0:256], (), ("FT" + R,), 256, ("b6",))
+            mv(T.FT[:, q4:q4 + 256], T.b6[0:64, 0:256], (), ("FT" + R,), 256, ("b6",))
             kb = 128 * r
             mm([(T.b6[:, 256 + 64 * j:320 + 64 * j], [(T.FT[:, q4 + 128 * j:q4 + 128 * j + 128], T.Rk[:, :]), (T.Ib[:, :], T.KB[:, kb + 64 * j:kb + 64 * j + 64])]) for j in (0, 1)],
                ("FT" + R, "Rk", "Ib", "KBa" + R, "KBb" + R), (), ("b6",))
@@ -338,19 +390,20 @@ def rank_program(g, core, T, topo):
             BA, BB = T.BI[:, 256 * t:256 * t + 128], T.BI[:, 256 * t + 128:256 * t + 256]
             mm([(T.b6[:, 384:448], [(BA, T.MK[:, q4 + 128:q4 + 192]), (BA, T.MK[:, q4 + 192:q4 + 256]), (BB, T.MK[:, q4 + 64:q4 + 128])]
                  + [(T.If[:, :], T.PRD[:, q4 + 64 * j:q4 + 64 * j + 64]) for j in range(4)])], mk + ("PRD" + R, "If", "BIa%d" % t, "BIb%d" % t), (), ("b6",), 200)
-            act(Pf, T.b6[:, 384:448], (), ("Pf" + R,), 64, ("b6",))
+            mv(Pf, T.b6[:, 384:448], (), ("Pf" + R,), 64, ("b6",))
             if t < 2:
                 cp(PL, T.b6[:, 384:448], (), ("PL" + R,), 64, ("b6",))
             else:
                 mm([(T.b6[0:64, 0:128], [(Pf, T.If[:, :])])], ("Pf" + R, "If"), (), ("b6",), 512)
                 act(T.PT[:, r::4], T.b6[0:64, 0:128], (), ("PT" + R,), 128, ("b6",), bias=-16.0)
+        mark[0] = 10 * t + 4
         rv = ("RV%d" % t,)
         mm([(T.b3[:, 64 * k:64 * k + 64], [(T.Ib[:, :], RV[:, :])]) for k in range(8)], rv + ("Ib",), (), ("b3",))
         for b in (0, 1):
-            tt(T.ler[:, 512 * b:512 * b + 512], T.f0[:, 512 * b:512 * b + 512], T.b3[:, :], OP.is_le, ("f00",), ("ler%d" % b,), 512, ("b3",))
-        cp(T.F[:, B + 256:B + 320], RV[:, :], rv, ("F%d4" % t,), 64, (), 0.5)
+            tt(T.ler[:, 512 * b:512 * b + 512], T.f0[:, 512 * b:512 * b + 512], T.b3[:, :], OP.is_le, ("f00%d" % b,), ("ler%d" % b,), 512, ("b3",))
+        mv(T.F[:, B + 256:B + 320], RV[:, :], rv, ("F%d4" % t,), 64)
         L4 = key(T.ler[:, :], ("ler0", "ler1"), 4)
-        gather("V", T.Sgs[:, 256:320], T.Sg[:, 0:1024], L4, ("Sg0", "L14"), ("Sgs4",), 64)
+        gather(T.Sgs[:, 256:320], T.Sg[:, 0:1024], L4, ("Sg00", "Sg01", "L14"), ("Sgs4",), 64)
         newsel(4, None, None, T.S[:, B + 256:B + 320], ("T%d4" % t,))
         fn = tuple("F%d%d" % (t, r) for r in range(5))
         sn = tuple("T%d%d" % (t, r) for r in range(5))
@@ -367,28 +420,8 @@ def rank_program(g, core, T, topo):
     succ = [[] for _ in range(n)]
     for k, o in enumerate(ops):
         for d in o["h"] | o["s"]: succ[d].append(k)
-    prio = [0.0] * n
-    for k in range(n - 1, -1, -1):
-        o = ops[k]
-        prio[k] = o["d"] + o["b"] + max([prio[s] + 0.08 for s in succ[k]], default=0.0)
-    left = [len(o["h"] | o["s"]) for o in ops]
-    free = {}
-    rdy = {k: 0.0 for k in range(n) if left[k] == 0}
-    order = []
-    while rdy:
-        est = {k: max(rdy[k], free.get(ops[k]["e"], 0.0)) for k in rdy}
-        lo = min(est.values())
-        k = max((k for k in rdy if est[k] <= lo + 0.05), key=lambda k: (prio[k], -k))
-        s = est[k]
-        isd = ops[k]["g"] is not None
-        free[ops[k]["e"]] = s + (0.1 if isd else ops[k]["d"])
-        if ops[k]["e"] == "N": free["N"] = 0.0
-        order.append(k)
-        del rdy[k]
-        for x in succ[k]:
-            left[x] -= 1
-            ops[x]["t"] = max(ops[x].get("t", 0.0), s + ops[k]["d"] + 0.08)
-            if left[x] == 0: rdy[x] = ops[x]["t"]
+    order, where, _ = schedule(ops, succ, MODEL, NOISE)
+    for k in range(n): ops[k]["e"] = where[k]
     sem = {e: T.sem["s" + e] for e in "VAPG"}
     queue = {"V": g.vector, "A": g.scalar, "P": g.tensor, "G": g, "Y": g.sync}
     gtot = {}
@@ -432,7 +465,8 @@ def rank_program(g, core, T, topo):
             def inc(i, e=e):
                 cnt[e] += 1
                 i.then_inc(sem[e], 1)
-            o["f"](inc)
+            if o["any"]: o["f"](inc, e)
+            else: o["f"](inc)
             done[k] = ("s" + e, cnt[e])
             know[k] = dict(seen[e])
             know[k]["s" + e] = cnt[e]

@@ -10,25 +10,25 @@ for _n, _c, _d in (
         ("f0", 4096, "bfloat16"), ("f1", 12288, "bfloat16"), ("Sg", 4096, "bfloat16"), ("le", 16384, "bfloat16"), ("ler", 1024, "bfloat16"),
         ("Gb", 256, "bfloat16"), ("Gr", 2048, "bfloat16"), ("Sgs", 320, "bfloat16"), ("QL", 768, "uint16"), ("Rl", 1024, "float32"),
         ("X", 1024, "float32"), ("X2", 512, "float32"), ("X3", 256, "float32"), ("XI", 256, "int32"), ("CI", 256, "int32"),
-        ("cb", 256, "bfloat16"), ("VT", 1024, "int32"), ("MK", 1024, "bfloat16"), ("PRD", 1024, "float32"), ("RI", 512, "int32"),
-        ("PL", 256, "uint16"), ("Pf", 256, "float32"), ("QE", 256, "uint16"), ("H", 2048, "bfloat16"), ("AC", 2048, "bfloat16"),
+        ("cb", 256, "bfloat16"), ("VT", 1024, "int32"), ("MK", 1024, "bfloat16"), ("PRD", 256, "float32"), ("PRB", 1024, "bfloat16"), ("RI", 512, "int32"),
+        ("PL", 256, "uint16"), ("Pf", 256, "float32"), ("QE", 256, "uint16"), ("H", 2048, "bfloat16"), ("H2", 2048, "bfloat16"), ("sA", 512, "bfloat16"), ("Ih", 128, "bfloat16"), ("thr", 2, "float32"), ("AC", 2048, "bfloat16"),
         ("A2", 1024, "bfloat16"), ("A3", 512, "bfloat16"), ("A4", 256, "bfloat16"), ("A5", 256, "bfloat16"),
         ("NF0", 64, "bfloat16"), ("NF1", 64, "bfloat16"), ("NF2", 64, "bfloat16"), ("RV0", 64, "bfloat16"), ("RV1", 64, "bfloat16"), ("RV2", 64, "bfloat16"),
         ("Mm", 40, "int32"), ("mi", 40, "int32"), ("L1", 40, "uint16"), ("mb", 32, "bfloat16"),
         ("sl", 196, "int32"), ("slf", 196, "float32"), ("slh", 196, "bfloat16"), ("sll", 196, "bfloat16"), ("LS", 200, "uint16"),
-        ("iu", 144, "float32"), ("ib", 128, "float32"), ("i16", 8, "float32"), ("pi", 1, "int32"), ("pii", 4, "int32"), ("pc", 16, "float32"),
-        ("Ib", 128, "bfloat16"), ("If", 128, "float32"), ("GA", 128, "bfloat16"), ("Sh", 128, "bfloat16"), ("In", 128, "bfloat16"),
+        ("iu", 144, "float32"), ("ib", 128, "float32"), ("i16", 8, "float32"), ("pi", 1, "int32"), ("pii", 4, "int32"), ("pc", 16, "float32"), ("pw", 8, "float32"),
+        ("Ib", 128, "bfloat16"), ("If", 128, "float32"), ("GA", 128, "bfloat16"), ("GI", 128, "bfloat16"), ("Sh", 128, "bfloat16"), ("In", 128, "bfloat16"),
         ("BI", 768, "bfloat16"), ("Z0", 144, "bfloat16"), ("Z1", 144, "bfloat16"), ("Z2", 144, "bfloat16"), ("Z3", 144, "bfloat16"),
-        ("K63", 64, "bfloat16"), ("Zh", 144, "bfloat16"), ("C512", 64, "bfloat16"), ("half", 1, "float32"), ("OFF", 192, "bfloat16"), ("ki", 768, "int32"), ("ki2", 768, "int32"), ("ki3", 768, "int32"), ("KB", 512, "bfloat16"),
+        ("K63", 64, "bfloat16"), ("Zh", 144, "bfloat16"), ("C512", 64, "bfloat16"), ("half", 1, "float32"), ("ki", 768, "int32"), ("ki2", 768, "int32"), ("ki3", 768, "int32"), ("KB", 512, "bfloat16"),
         ("gi", 384, "int32"), ("gi2", 384, "int32"), ("GM", 384, "bfloat16"), ("Ys", 8, "bfloat16"),
-        ("vh", 256, "float32"), ("VH", 256, "bfloat16"), ("VL", 256, "bfloat16")):
+        ("vh", 256, "float32"), ("VH", 256, "bfloat16"), ("VL", 256, "bfloat16"), ("V8", 256, "bfloat16")):
     SCRATCH[_n] = ("sbuf", [128, _c], _d)
 SCRATCH["PS"] = ("sbuf", [64, 512], "int32")
 SCRATCH["PSf"] = ("sbuf", [64, 512], "float32")
 SCRATCH["PT"] = ("sbuf", [64, 512], "float32")
-SCRATCH["FT"] = ("sbuf", [64, 1024], "bfloat16")
-SCRATCH["Rk"] = ("sbuf", [64, 64], "bfloat16")
-SCRATCH["irk"] = ("sbuf", [64, 64], "float32")
+SCRATCH["FT"] = ("sbuf", [128, 512], "bfloat16")
+SCRATCH["Rk"] = ("sbuf", [128, 128], "bfloat16")
+SCRATCH["irk"] = ("sbuf", [128, 128], "float32")
 SCRATCH["mT"] = ("sbuf", [4, 512], "bfloat16")
 SCRATCH["SS"] = ("sbuf", [49, 512], "int32")
 SCRATCH["SSf"] = ("sbuf", [49, 512], "float32")
@@ -38,10 +38,20 @@ for _k in range(8):
 GROUPS = ["dpar", "dsel", "dsl", "dfr", "dsw", "ds0", "ds1", "ds2", "ds3", "doutf", "douts", "doutp"]
 SEMAPHORES = ["sV", "sA", "sP", "sG", "rv0", "rv1", "rv2", "ls"] + GROUPS
 ENG = ("V", "A", "P", "G", "Y")
-MODES = ("CSFF", "SFFF", "SCFF", "CSSF")
+MODES = ("SCFF", "SFFF", "SCFF", "SSCF")
+CF = {"HM": "FFFA", "f0": 2, "Sg": 2, "fh": 2, "SZ": "G", "CB": "A"}
 CY = 0.00095
-MODEL = {"cy": 0.00095, "gam": 1.56, "pe": 0.00045, "sem": 0.07, "eps": 0.05, "chunk": 0.0, "vb": 1.0}
-NOISE = None
+MODEL = {"cy": 0.00095, "gam": 1.5, "pe": 0.00045, "sem": 0.061, "eps": 0.014, "chunk": 0.0, "vb": 0.86, "vg": 0.45}
+SEEDS = [(735020, 2, 0.005), (748862, 0.5, 0.01), (94243, 1, 0.005), (242009, 1, 0.005), (385449, 0.5, 0.005), (234413, 1, 0.005), (385998, 4, 0.005),
+         (526160, 0.5, 0.005), (749604, 2, 0.005), (130020, 1, 0.01), (86384, 0.5, 0.005)]
+
+
+def spread(n):
+    z = np.zeros(n)
+    for s, amp, frac in SEEDS:
+        g = np.random.default_rng(s)
+        z += np.where(g.random(n) < frac, (g.random(n) - 0.5) * amp, 0.0)
+    return [float(x) for x in z]
 
 
 def schedule(ops, succ, M, noise=None):
@@ -64,13 +74,16 @@ def schedule(ops, succ, M, noise=None):
         est = []
         for k in rdy:
             e = where[k]
-            if e == "*": e = "V" if max(at[k], free["V"]) + M["vb"] < max(at[k], free["A"]) else "A"
+            if e == "*":
+                e = "V" if max(at[k], free["V"]) + M["vb"] < max(at[k], free["A"]) else "A"
+                if "gc" in ops[k] and max(at[k], free["G"]) + ops[k]["gc"] < max(at[k], free[e]) + d[k] + M["vg"]: e = "G"
             s = max(at[k], free[e])
             est.append((k, e, s))
             if s < lo: lo = s
         k, e, s = max((x for x in est if x[2] <= lo + M["eps"]), key=lambda x: (prio[x[0]], -x[0]))
         where[k] = e
-        if e != "N": free[e] = s + (0.1 if ops[k]["g"] is not None else d[k])
+        if e == "G" and "gc" in ops[k]: d[k] = ops[k]["gc"]
+        if e != "N": free[e] = s + (0.1 if ops[k]["g"] is not None and ops[k]["g"] != "send" else d[k])
         order.append(k)
         rdy.remove(k)
         end = max(end, s + d[k])
@@ -117,6 +130,13 @@ def rank_program(g, core, T, topo):
     def gather(out, win, off, r, w, n):
         op("*", lambda inc, e: inc(V.tensor_copy(out, win.indirect(off)) if e == "V" else A.activation(out, win.indirect(off), AF.Copy)), r, w, gd(n))
 
+    def mg(out, i0, r, w, n):
+        def fn(inc, e):
+            if e == "G": inc(g.affine_select(out, i0, [[0, n]], OP.is_ge, 0.0, 0, 0))
+            else: inc(V.tensor_copy(out, i0) if e == "V" else A.activation(out, i0, AF.Copy))
+        k = op("*", fn, r, w, (0.03, max(64, n * 0.75), 0, 0))
+        ops[k]["gc"] = 0.17 + 2 * n * CY
+
     def mv(out, i0, r=(), w=(), n=64, ps=(), h=1.0):
         op("*", lambda inc, e: inc(V.tensor_copy(out, i0) if e == "V" else A.activation(out, i0, AF.Copy)), r, w, ad(n), ps)
 
@@ -161,23 +181,25 @@ def rank_program(g, core, T, topo):
     iota(T.pi[:, :], [[0, 1]], 0, 1, ("pi",), 1, False)
     iota(T.iu[:, :], [[1, 144]], 0, 0, ("iu",), 144)
     iota(T.ib[:, :], [[0, 8], [1, 16]], 0, 0, ("ib",), 128)
-    iota(T.irk[:, :], [[0, 16], [1, 4]], 0, 0, ("irk",), 64)
+    iota(T.irk[:, :], [[0, 32], [1, 4]], 0, 0, ("irk",), 128)
     iota(T.vh[:, :], [[16, 16], [0, 16]], 16, 0, ("vh",), 256)
     iota(T.VL[:, :], [[0, 16], [1, 16]], 0, 0, ("VL",), 256)
+    iota(T.V8[:, :], [[0, 256]], 8192, 0, ("V8",), 256)
     iota(T.K63[:, :], [[-1, 64]], 63, 0, ("K63",), 64)
     iota(T.i16[:, :], [[16, 8]], 15, 0, ("i16",), 8)
     iota(T.ki[:, 0:256], [[1, 4], [1, 16], [64, 4]], 0, 0, ("ki0",), 256, False)
-    iota(T.ki[:, 256:512], [[5, 4], [37, 16], [320, 4]], 0, 0, ("ki1",), 256, False)
+    iota(T.ki[:, 256:512], [[5, 4], [37, 16], [320, 4]], 16 if CF["CB"] == "A" else 0, 0, ("ki1",), 256, False)
     iota(T.ki[:, 512:768], [[1, 4], [0, 16], [64, 4]], 0, 0, ("ki2",), 256, False)
     iota(T.gi[:, :], [[1, 6], [0, 16], [4, 4]], 0, 0, ("gi",), 384, False)
     fill(T.F[:, 0:16], 0.0, ("Fz",), 16)
     fill(T.SELw[:, :], 0.0, ("SELw",), 3152)
     early[0] = -6.0
-    for k in range(8): fill(T.S[:, 514 * k:514 * k + 514], 0.0, ("Sz%d" % k,), 514)
+    for k in range(8):
+        if CF["SZ"] == "V": fill(T.S[:, 514 * k:514 * k + 514], 0.0, ("Sz%d" % k,), 514)
+        else: iota(T.S[:, 514 * k:514 * k + 514], [[0, 514]], 0, 0, ("Sz%d" % k,), 514)
     early[0] = 0.0
     Sz = tuple("Sz%d" % k for k in range(8))
     fill(T.C1[:, 0:16], 0.0, ("C1z",), 16)
-    for k in range(3): fill(T.OFF[:, 64 * k:64 * k + 64], 8192.0 * (k + 1), ("OFF%d" % k,), 64)
     ts(T.pii[:, 0:1], T.pi[:, :], 15, None, OP.bitwise_and, r=("pi",), w=("pii0",))
     ts(T.pii[:, 1:2], T.pi[:, :], 15, 1, OP.bitwise_and, OP.arith_shift_right, r=("pi",), w=("pii1",))
     ts(T.pii[:, 2:3], T.pi[:, :], 3, None, OP.bitwise_and, r=("pi",), w=("pii2",))
@@ -188,6 +210,9 @@ def rank_program(g, core, T, topo):
     ts(T.pc[:, 3:4], T.pc[:, 1:2], 1008.0, None, OP.add, r=("pc1",), w=("pc3",))
     cp(T.pc[:, 4:5], T.pii[:, 1:2], ("pii1",), ("pc4",))
     for k in (1, 2, 3): ts(T.pc[:, 4 + k:5 + k], T.pc[:, 4:5], float(k), None, OP.is_equal, r=("pc4",), w=("pc%d" % (4 + k),))
+    for k in (1, 2, 3):
+        ts(T.pw[:, 3 + k:4 + k], T.pc[:, 1:2], 8.0, float(k), OP.is_equal, OP.mult, r=("pc1",), w=("pv%d" % k,))
+        tt(T.pw[:, k:k + 1], T.pw[:, 3 + k:4 + k], T.pc[:, 4 + k:5 + k], OP.add, ("pv%d" % k, "pc%d" % (4 + k)), ("pw%d" % k,), 64)
     ts(T.pc[:, 8:9], T.pc[:, 1:2], 256.0, None, OP.mult, r=("pc1",), w=("pc8",))
     ts(T.pc[:, 10:11], T.pc[:, 4:5], 3.0, None, OP.is_lt, r=("pc4",), w=("pc10",))
     cp(T.pc[:, 11:12], T.pii[:, 2:3], ("pii2",), ("pc11",))
@@ -201,14 +226,21 @@ def rank_program(g, core, T, topo):
     fill(T.C512[:, :], 512.0, ("C512",), 64)
     fill(T.half[:, :], 0.5, ("half",), 1)
     for k in (1, 2, 3):
-        ts(T["Z%d" % k][:, :], T.iu[:, :], T.pc[:, 2:3], T.pc[:, 4 + k:5 + k], OP.is_equal, OP.mult, r=("iu", "pc2", "pc%d" % (4 + k)), w=("Z%d" % k,), n=144)
+        ts(T["Z%d" % k][:, :], T.iu[:, :], T.pc[:, 2:3], T.pw[:, k:k + 1], OP.is_equal, OP.mult, r=("iu", "pc2", "pw%d" % k), w=("Z%d" % k,), n=144)
     ts(T.GA[:, :], T.ib[:, :], T.pc[:, 1:2], None, OP.is_equal, r=("ib", "pc1"), w=("GA",), n=128)
+    if CF["CB"] == "A":
+        tt(T.GI[:, :], T.GA[:, :], T.Ib[:, :], OP.add, ("GA", "Ib"), ("GI",), 128)
+        mv2 = lambda inc: inc(A.activation(T.Ih[:, :], T.Ib[:, :], AF.Copy, scale=0.5))
+        op("A", mv2, ("Ib",), ("Ih",), ad(128))
+        for j in (0, 1): fill(T.thr[:, j:j + 1], -(16383.5 + 8192 * j), ("thr%d" % j,), 1)
     ts(T.Sh[:, :], T.iu[:, 0:128], T.pc[:, 15:16], T.pc[:, 10:11], OP.is_equal, OP.mult, r=("iu", "pc15", "pc10"), w=("Sh",), n=128)
     ts(T.In[:, :], T.Ib[:, :], -1.0, None, OP.mult, r=("Ib",), w=("In",), n=128, c=0.5)
     for k in range(3):
         ts(T.BI[:, 256 * k:256 * k + 128], T.Ib[:, :], float(B0 + 320 * k), None, OP.mult, r=("Ib",), w=("BIa%d" % k,), n=128, c=0.5)
         ts(T.BI[:, 256 * k + 128:256 * k + 256], T.Ib[:, :], float(B0 + 320 * k + 256), None, OP.mult, r=("Ib",), w=("BIb%d" % k,), n=128, c=0.5)
-    ts(T.Rk[:, :], T.irk[:, :], T.pc[0:64, 11:12], None, OP.is_equal, r=("irk", "pc11"), w=("Rk",))
+    ts(T.Rk[:, :], T.irk[:, :], T.pc[:, 11:12], None, OP.is_equal, r=("irk", "pc11"), w=("Rk",), n=128)
+    op("V", lambda inc: inc(V.memset(T.Rk[0:64, 64:128], 0.0)), (), ("Rk", "Rky"), vd(64))
+    op("V", lambda inc: inc(V.memset(T.Rk[64:128, 0:64], 0.0)), ("Rky",), ("Rk", "Rkz"), vd(64))
     ts(T.Ys[:, :], T.i16[:, :], T.pc[:, 2:3], T.pc[:, 5:6], OP.is_equal, OP.mult, r=("i16", "pc2", "pc5"), w=("Ys",))
     ts(T.ki2[:, 0:256], T.ki[:, 0:256], T.pc[:, 13:14], None, OP.add, r=("ki0", "pc13"), w=("kj0",), n=256)
     ts(T.ki2[:, 256:512], T.ki[:, 256:512], T.pc[:, 12:13], None, OP.add, r=("ki1", "pc12"), w=("kj1",), n=256)
@@ -223,6 +255,7 @@ def rank_program(g, core, T, topo):
     op("A", lambda inc: inc(A.activation(T.VH[:, :], T.vh[:, :], AF.Identity, bias=T.pc[:, 8:9])), ("vh", "pc8"), ("VH",), ad(256))
     dma("Y", T.S[0::16, 16:4112], T.VH[:, :], "ds0", ("VH",) + Sz, ("S0",))
     dma("Y", T.S[1::16, 16:4112], T.VL[:, :], "ds0", ("VL",) + Sz, ("S1",))
+    dma("Y", T.S[8::16, 16:4112], T.V8[:, :], "ds0", ("V8",) + Sz, ("S8",))
     Sv = Sz
     ts(T.PSf[:, :], T.PS[:, :], 16.0, None, OP.add, r=tuple("PS%d" % k for k in range(8)), w=("PSf",), n=512)
     mm([(T.b6[:, 64 * r:64 * r + 64], [(T.PSf[:, r::4], T.If[0:64, 0:64])]) for r in range(4)], ("PSf", "If"), (), ("b6",), 256)
@@ -248,8 +281,8 @@ def rank_program(g, core, T, topo):
         dma("Y", T.S[4 + k::16, 16:B0], T.C1[2 + k::16, 16:B0], "ds2", c1 + Sv, ("S%d" % (4 + k),))
     for k in (0, 1):
         dma("Y", T.S[6 + k::16, 16:B0], T.C2[2 + k::16, 16:B0], "ds3", c2 + Sv, ("S%d" % (6 + k),))
-    Sr = Sv + tuple("S%d" % k for k in range(8))
-    Sv = Sz + ("S0", "S1")
+    Sr = Sv + tuple("S%d" % k for k in range(9))
+    Sv = Sz + ("S0", "S1", "S8")
     Fr = ("Fi", "Fz")
 
     def z(n, y): return T["Z%s" % n][:, 15 - y:143 - y]
@@ -278,32 +311,33 @@ def rank_program(g, core, T, topo):
             PL, Pf = T.PL[:, q0:q0 + 64], T.Pf[:, q0:q0 + 64]
             f0, f1, Sg = T.f0[:, 1024 * r:1024 * r + 1024], T.f1[:, 1024 * r:1024 * r + 1024], T.Sg[:, 1024 * r:1024 * r + 1024]
             mark[0] = 10 * t + r
-            for b in (0, 1):
-                gather(f0[:, 512 * b:512 * b + 512], win, PL[:, 32 * b:32 * b + 32], Fr + ("PL" + R,), ("f0%d%d" % (r, b),), 512)
-            for b in (0, 1):
-                gather(Sg[:, 512 * b:512 * b + 512], swin, PL[:, 32 * b:32 * b + 32], Sr + ("PL" + R,), ("Sg%d%d" % (r, b),), 512)
+            def gath(out, wn, lists, rk, name, parts):
+                for b in range(parts):
+                    n_ = 1024 // parts
+                    gather(out[:, n_ * b:n_ * b + n_], wn, lists[:, n_ // 16 * b:n_ // 16 * (b + 1)], rk,
+                           (name + "%d%d" % (r, b),) if parts == 2 else (name + "%d0" % r, name + "%d1" % r), n_)
+            gath(f0, win, PL, Fr + ("PL" + R,), "f0", CF["f0"])
+            gath(Sg, swin, PL, Sr + ("PL" + R,), "Sg", CF["Sg"])
             f0k, Sgk = ("f0%d0" % r, "f0%d1" % r), ("Sg%d0" % r, "Sg%d1" % r)
             L1 = key(f0, f0k, r)
             gather(T.Gb[:, q0:q0 + 64], f0, L1, f0k + ("L1" + R,), ("Gb" + R,), 64)
             g5 = 512 * r
-            mv(T.Gr[:, g5:g5 + 64], T.Gb[:, q0:q0 + 64], ("Gb" + R,), ("Gra" + R,), 64)
-            mv(T.Gr[:, g5 + 64:g5 + 128], T.Gb[:, q0:q0 + 64], ("Gb" + R,), ("Grb" + R,), 64)
-            mv(T.Gr[:, g5 + 128:g5 + 256], T.Gr[:, g5:g5 + 128], ("Gra" + R, "Grb" + R), ("Grc" + R,), 128)
-            mv(T.Gr[:, g5 + 256:g5 + 512], T.Gr[:, g5:g5 + 256], ("Gra" + R, "Grb" + R, "Grc" + R), ("Grd" + R,), 256)
+            mg(T.Gr[:, g5:g5 + 64], T.Gb[:, q0:q0 + 64], ("Gb" + R,), ("Gra" + R,), 64)
+            mg(T.Gr[:, g5 + 64:g5 + 128], T.Gb[:, q0:q0 + 64], ("Gb" + R,), ("Grb" + R,), 64)
+            mg(T.Gr[:, g5 + 128:g5 + 256], T.Gr[:, g5:g5 + 128], ("Gra" + R, "Grb" + R), ("Grc" + R,), 128)
+            mg(T.Gr[:, g5 + 256:g5 + 512], T.Gr[:, g5:g5 + 256], ("Gra" + R, "Grb" + R, "Grc" + R), ("Grd" + R,), 256)
             Gk = tuple("Gr%s%d" % (x, r) for x in "abcd")
             MD = MODES[r]
             mm([(Q[:, 0:64], [(T.If[:, :], Pf)])], ("Pf" + R, "If"), (), (Qb,), 256)
             for h in (1, 2, 3):
-                mm([(Q[:, 64 * h:64 * h + 64], [(z(h, y), Sg[:, y::16]) for y in range(16)] + [(T.Ib[:, :], T.OFF[:, 64 * h - 64:64 * h])])],
-                   Sgk + ("Z%d" % h, "Ib", "OFF%d" % (h - 1)), (), (Qb,))
+                mm([(Q[:, 64 * h:64 * h + 64], [(z(h, y), Sg[:, y::16]) for y in range(16)])], Sgk + ("Z%d" % h,), (), (Qb,))
             for h in (1, 2, 3):
                 a = 192 * r + 64 * h - 64
                 ts(T.QL[:, a:a + 64], Q[:, 64 * h:64 * h + 64], -8192.0 * h, None, OP.add, w=("QL%d%d" % (r, h),), ps=(Qb,))
             fh = [f0] + [T.f1[:, 4096 * (h - 1) + 1024 * r:4096 * (h - 1) + 1024 * r + 1024] for h in (1, 2, 3)]
             for h in (1, 2, 3):
-                for b in (0, 1):
-                    a = 192 * r + 64 * h - 64 + 32 * b
-                    if MD[h] != "F": gather(fh[h][:, 512 * b:512 * b + 512], win, T.QL[:, a:a + 32], Fr + ("QL%d%d" % (r, h),), ("f%d%d%d" % (h, r, b),), 512)
+                a = 192 * r + 64 * h - 64
+                if MD[h] != "F": gath(fh[h], win, T.QL[:, a:a + 64], Fr + ("QL%d%d" % (r, h),), "f%d" % h, CF["fh"])
             gather(T.Sgs[:, q0:q0 + 64], Sg, L1, Sgk + ("L1" + R,), ("Sgs" + R,), 64)
             for h in range(4):
                 if MD[h] == "C": mm([(GP[:, :], [(T.Ib[:, :], T.Gr[:, g5:g5 + 512])])], Gk + ("Ib",), (), (GPb,), 512)
@@ -336,7 +370,11 @@ def rank_program(g, core, T, topo):
             for b in (1, 0):
                 hb = h5 + 256 * b
                 gather(T.H[:, hb:hb + 256], win, T.QE[:, q0 + 32 + 16 * b:q0 + 48 + 16 * b], Fr + ("QE" + R,), ("H%d%d" % (r, b),), 256)
-                op("V", lambda inc, hb=hb, a=q0 + 16 * b, win=win: inc(V.tensor_tensor(T.AC[:, hb:hb + 256], win.indirect(T.QE[:, a:a + 16]), T.H[:, hb:hb + 256], OP.max)),
+                if CF["HM"][r] == "A":
+                    gather(T.H2[:, hb:hb + 256], win, T.QE[:, q0 + 16 * b:q0 + 16 + 16 * b], Fr + ("QE" + R,), ("H2%d%d" % (r, b),), 256)
+                    mm([(T.b7[:, 0:256], [(T.Ib[:, :], T.H[:, hb:hb + 256])])], ("H%d%d" % (r, b), "Ib"), (), ("b7",), 256)
+                    tt(T.AC[:, hb:hb + 256], T.H2[:, hb:hb + 256], T.b7[:, 0:256], OP.max, ("H2%d%d" % (r, b),), ("AC%d%d" % (r, b),), 256, ("b7",))
+                else: op("V", lambda inc, hb=hb, a=q0 + 16 * b, win=win: inc(V.tensor_tensor(T.AC[:, hb:hb + 256], win.indirect(T.QE[:, a:a + 16]), T.H[:, hb:hb + 256], OP.max)),
                    Fr + ("QE" + R, "H%d%d" % (r, b)), ("AC%d%d" % (r, b),), gd(256))
                 if b: mm([(T.b7[:, 256:512], [(T.Ib[:, :], T.AC[:, hb:hb + 256])])], ("AC%d1" % r, "Ib"), (), ("b7",), 256)
             tt(T.b7[:, 128:256], T.AC[:, h5 + 128:h5 + 256], T.b7[:, 384:512], OP.max, ("AC%d0" % r,), ("AP",), 128, ("b7",))
@@ -360,7 +398,7 @@ def rank_program(g, core, T, topo):
                     g.remote_dma(RV[:, :], NF[:, :], T.sem["rv%d" % t], T.sem["ls"], pid, rid, sum(1 << e for e in ne))
                 op("G", send, ("NF%d" % t,), ("sent%d" % t,), 1.5, grp="send")
                 op("N", ("rv%d" % t, nr), ("sent%d" % t,), ("RV%d" % t,), 2.5)
-                mv(T.F[:, B + r:B + 256:4], NF[:, :], ("NF%d" % t,), (fk,), 64)
+                mg(T.F[:, B + r:B + 256:4], NF[:, :], ("NF%d" % t,), (fk,), 64)
             else:
                 ts(T.F[:, B + r:B + 256:4], T.A5[:, q0:q0 + 64], 255.0, None, OP.min, r=("A5" + R,), w=(fk,), c=0.5)
             newsel(r, r, None, T.S[:, B + r:B + 256:4], ("T%d%d" % (t, r),))
@@ -368,28 +406,40 @@ def rank_program(g, core, T, topo):
             cp(T.mb[:, m4:m4 + 4], T.mi[:, m4:m4 + 4], ("mi" + R,), ("mb" + R,))
             mm([(T.b6[0:4, 256:384], [(T.mb[:, m4:m4 + 4], T.Ib[:, :])])], ("mb" + R, "Ib"), (), ("b6",), 128)
             mv(T.mT[:, 128 * r:128 * r + 128], T.b6[0:4, 256:384], (), ("mT" + R,), 128, ("b6",))
-            mm([(T.b6[:, 0:64], [(T.mT[:, 128 * r:128 * r + 128], T.Rk[0:4, :]), (T.In[:, :], T.K63[:, :])])], ("mT" + R, "Rk", "In", "K63"), (), ("b6",))
+            mm([(T.b6[:, 0:64], [(T.mT[:, 128 * r:128 * r + 128], T.Rk[0:4, 0:64]), (T.In[:, :], T.K63[:, :])])], ("mT" + R, "Rk", "In", "K63"), (), ("b6",))
             ts(T.MK[:, q4 + 192:q4 + 256], T.b6[:, 0:64], 0.0, None, OP.is_equal, w=("MKs" + R,), ps=("b6",))
             ts(T.MK[:, q4:q4 + 64], T.X3[:, q0:q0 + 64], 8192.0, None, OP.is_ge, r=("X3" + R,), w=("MKn" + R,))
             ts(T.MK[:, q4 + 128:q4 + 192], T.X3[:, q0:q0 + 64], 32768.0, None, OP.is_ge, r=("X3" + R,), w=("MKr" + R,))
-            ts(T.CI[:, q0:q0 + 64], T.XI[:, q0:q0 + 64], 13, None, OP.arith_shift_right, r=("XI" + R,), w=("CI" + R,))
-            cp(T.cb[:, q0:q0 + 64], T.CI[:, q0:q0 + 64], ("CI" + R,), ("cb" + R,))
+            if CF["CB"] == "V":
+                ts(T.CI[:, q0:q0 + 64], T.XI[:, q0:q0 + 64], 13, None, OP.arith_shift_right, r=("XI" + R,), w=("CI" + R,))
+                cp(T.cb[:, q0:q0 + 64], T.CI[:, q0:q0 + 64], ("CI" + R,), ("cb" + R,))
+            else:
+                for j in (0, 1):
+                    op("A", lambda inc, j=j, q0=q0: inc(A.activation(T.sA[:, 2 * q0 + 64 * j:2 * q0 + 64 * j + 64], T.X3[:, q0:q0 + 64], AF.Sign, bias=T.thr[:, j:j + 1])),
+                       ("X3" + R, "thr%d" % j), ("sA%d%d" % (r, j),), ad(64))
             tt(T.MK[:, q4 + 64:q4 + 128], T.MK[:, q4:q4 + 64], T.MK[:, q4 + 192:q4 + 256], OP.is_equal, ("MKn" + R, "MKs" + R), ("MK0" + R,), 64)
             red, cb = T.MK[:, q4 + 128:q4 + 192], T.cb[:, q0:q0 + 64]
-            mm([(T.b6[0:64, 0:128], [(red, T.GA[:, :])]), (T.b6[0:64, 128:256], [(red, T.GA[:, :]), (cb, T.Ib[:, :])])], ("MKr" + R, "cb" + R, "GA", "Ib"), (), ("b6",), 128)
-            mv(T.FT[:, q4:q4 + 256], T.b6[0:64, 0:256], (), ("FT" + R,), 256, ("b6",))
+            if CF["CB"] == "V":
+                mm([(T.b6[0:64, 0:128], [(red, T.GA[:, :])]), (T.b6[64:128, 0:128], [(red, T.GA[:, :]), (cb, T.Ib[:, :])])], ("MKr" + R, "cb" + R, "GA", "Ib"), (), ("b6",), 128)
+            else:
+                mm([(T.b6[0:64, 0:128], [(red, T.GA[:, :])]),
+                    (T.b6[64:128, 0:128], [(red, T.GI[:, :]), (T.MK[:, q4:q4 + 64], T.Ib[:, :])] + [(T.sA[:, 2 * q0 + 64 * j:2 * q0 + 64 * j + 64], T.Ih[:, :]) for j in (0, 1)])],
+                   ("MKr" + R, "MKn" + R, "sA%d0" % r, "sA%d1" % r, "GA", "GI", "Ib", "Ih"), (), ("b6",), 128)
             kb = 128 * r
-            mm([(T.b6[:, 256 + 64 * j:320 + 64 * j], [(T.FT[:, q4 + 128 * j:q4 + 128 * j + 128], T.Rk[:, :]), (T.Ib[:, :], T.KB[:, kb + 64 * j:kb + 64 * j + 64])]) for j in (0, 1)],
-               ("FT" + R, "Rk", "Ib", "KBa" + R, "KBb" + R), (), ("b6",))
+            mv(T.FT[:, kb:kb + 128], T.b6[:, 0:128], (), ("FT" + R,), 128, ("b6",))
+            mm([(T.b6[:, 256:384], [(T.FT[:, kb:kb + 128], T.Rk[:, :]), (T.Ib[:, :], T.KB[:, kb:kb + 128])])],
+               ("FT" + R, "Rk", "Rkz", "Ib", "KBa" + R, "KBb" + R), (), ("b6",), 128)
             cp(T.RI[:, kb:kb + 128], T.b6[:, 256:384], (), ("RI" + R,), 128, ("b6",))
             ts(T.VT[:, q4 + 64:q4 + 128], T.RI[:, kb:kb + 64], 63, None, OP.bitwise_and, r=("RI" + R,), w=("VTb" + R,))
             ts(T.VT[:, q4 + 128:q4 + 192], T.RI[:, kb + 64:kb + 128], 255, None, OP.bitwise_and, r=("RI" + R,), w=("VTa" + R,))
             mk = ("MKn" + R, "MK0" + R, "MKr" + R, "MKs" + R)
             mm([(T.b6[:, 0:256], [(T.Ib[:, :], T.MK[:, q4:q4 + 256])])], mk + ("Ib",), (), ("b6",), 256)
-            tt(T.PRD[:, q4:q4 + 256], T.VT[:, q4:q4 + 256], T.b6[:, 0:256], OP.mult, ("VTq" + R, "VTb" + R, "VTa" + R, "VTi" + R), ("PRD" + R,), 256, ("b6",))
+            tt(T.PRD[:, q0:q0 + 64], T.VT[:, q4:q4 + 64], T.b6[:, 0:64], OP.mult, ("VTq" + R,), ("PRD" + R,), 64, ("b6",))
+            tt(T.PRB[:, q4:q4 + 192], T.VT[:, q4 + 64:q4 + 256], T.b6[:, 64:256], OP.mult, ("VTb" + R, "VTa" + R, "VTi" + R), ("PRB" + R,), 192, ("b6",))
             BA, BB = T.BI[:, 256 * t:256 * t + 128], T.BI[:, 256 * t + 128:256 * t + 256]
             mm([(T.b6[:, 384:448], [(BA, T.MK[:, q4 + 128:q4 + 192]), (BA, T.MK[:, q4 + 192:q4 + 256]), (BB, T.MK[:, q4 + 64:q4 + 128])]
-                 + [(T.If[:, :], T.PRD[:, q4 + 64 * j:q4 + 64 * j + 64]) for j in range(4)])], mk + ("PRD" + R, "If", "BIa%d" % t, "BIb%d" % t), (), ("b6",), 200)
+                 + [(T.Ib[:, :], T.PRB[:, q4 + 64 * j:q4 + 64 * j + 64]) for j in range(3)] + [(T.If[:, :], T.PRD[:, q0:q0 + 64])])],
+               mk + ("PRD" + R, "PRB" + R, "If", "Ib", "BIa%d" % t, "BIb%d" % t), (), ("b6",), 92)
             mv(Pf, T.b6[:, 384:448], (), ("Pf" + R,), 64, ("b6",))
             if t < 2:
                 cp(PL, T.b6[:, 384:448], (), ("PL" + R,), 64, ("b6",))
@@ -401,7 +451,7 @@ def rank_program(g, core, T, topo):
         mm([(T.b3[:, 64 * k:64 * k + 64], [(T.Ib[:, :], RV[:, :])]) for k in range(8)], rv + ("Ib",), (), ("b3",))
         for b in (0, 1):
             tt(T.ler[:, 512 * b:512 * b + 512], T.f0[:, 512 * b:512 * b + 512], T.b3[:, :], OP.is_le, ("f00%d" % b,), ("ler%d" % b,), 512, ("b3",))
-        mv(T.F[:, B + 256:B + 320], RV[:, :], rv, ("F%d4" % t,), 64)
+        mg(T.F[:, B + 256:B + 320], RV[:, :], rv, ("F%d4" % t,), 64)
         L4 = key(T.ler[:, :], ("ler0", "ler1"), 4)
         gather(T.Sgs[:, 256:320], T.Sg[:, 0:1024], L4, ("Sg00", "Sg01", "L14"), ("Sgs4",), 64)
         newsel(4, None, None, T.S[:, B + 256:B + 320], ("T%d4" % t,))
@@ -414,13 +464,13 @@ def rank_program(g, core, T, topo):
         act(T.ysb[:, 320 * t:320 * t + 320], T.b7[0:8, 0:320], (), ("ysb%d" % t,), 320, ("b7",), bias=-16.0)
         dma("Y", T.ys[:, 320 * t:320 * t + 320], T.ysb[:, 320 * t:320 * t + 320], "douts", ("ysb%d" % t,))
     for k in range(8):
-        dma("Y", T.yp[16 * k:16 * k + 16, :], T.PT[:, 64 * k:64 * k + 64], "doutp", tuple("PT%d" % r for r in range(4)))
+        dma("YA"[k % 2], T.yp[16 * k:16 * k + 16, :], T.PT[:, 64 * k:64 * k + 64], "doutp", tuple("PT%d" % r for r in range(4)))
 
     n = len(ops)
     succ = [[] for _ in range(n)]
     for k, o in enumerate(ops):
         for d in o["h"] | o["s"]: succ[d].append(k)
-    order, where, _ = schedule(ops, succ, MODEL, NOISE)
+    order, where, _ = schedule(ops, succ, MODEL, spread(n))
     for k in range(n): ops[k]["e"] = where[k]
     sem = {e: T.sem["s" + e] for e in "VAPG"}
     queue = {"V": g.vector, "A": g.scalar, "P": g.tensor, "G": g, "Y": g.sync}

import numpy as np
from concourse.bass import DstId, RemoteDMATransfer
from concourse.mybir import dt, AluOpType, AxisListType, ActivationFunctionType

OP = AluOpType
AF = ActivationFunctionType
SCRATCH = {}
for _n, _c, _d in (
        ("F", 4112, "bfloat16"), ("S", 4112, "bfloat16"), ("SELw", 3152, "bfloat16"), ("C1", 3152, "bfloat16"), ("C2", 3152, "bfloat16"),
        ("f0", 4096, "bfloat16"), ("f1", 12288, "bfloat16"), ("Sg", 4096, "bfloat16"), ("le", 16384, "bfloat16"), ("ler", 1024, "bfloat16"),
        ("Gb", 256, "bfloat16"), ("Gr", 2048, "bfloat16"), ("Sgs", 320, "bfloat16"), ("QL", 768, "uint16"), ("Rl", 1024, "float32"),
        ("X", 1024, "float32"), ("X2", 512, "float32"), ("X3", 256, "float32"), ("XI", 256, "int32"), ("CI", 256, "int32"),
        ("cb", 256, "bfloat16"), ("VT", 1024, "int32"), ("MK", 1024, "bfloat16"), ("PRD", 256, "float32"), ("PRB", 1024, "bfloat16"), ("RI", 512, "int32"),
        ("PL", 256, "uint16"), ("Pf", 256, "float32"), ("QE", 256, "uint16"), ("H", 2048, "bfloat16"), ("H2", 2048, "bfloat16"), ("sA", 512, "bfloat16"), ("Ih", 128, "bfloat16"), ("thr", 2, "float32"), ("AC", 2048, "bfloat16"),
        ("A2", 1024, "bfloat16"), ("A3", 512, "bfloat16"), ("A4", 256, "bfloat16"), ("A5", 256, "bfloat16"),
        ("NF0", 64, "bfloat16"), ("NF1", 64, "bfloat16"), ("NF2", 64, "bfloat16"), ("RV0", 64, "bfloat16"), ("RV1", 64, "bfloat16"), ("RV2", 64, "bfloat16"),
        ("Mm", 40, "int32"), ("mi", 40, "int32"), ("L1", 40, "uint16"), ("mb", 32, "bfloat16"),
        ("sl", 196, "int32"), ("slf", 196, "float32"), ("slh", 196, "bfloat16"), ("sll", 196, "bfloat16"), ("LS", 200, "uint16"),
        ("iu", 144, "float32"), ("ib", 128, "float32"), ("i16", 8, "float32"), ("pi", 1, "int32"), ("pii", 4, "int32"), ("pc", 16, "float32"), ("pw", 8, "float32"),
        ("Ib", 128, "bfloat16"), ("If", 128, "float32"), ("GA", 128, "bfloat16"), ("GI", 128, "bfloat16"), ("Sh", 128, "bfloat16"), ("In", 128, "bfloat16"),
        ("BI", 768, "bfloat16"), ("Z0", 144, "bfloat16"), ("Z1", 144, "bfloat16"), ("Z2", 144, "bfloat16"), ("Z3", 144, "bfloat16"),
        ("K63", 64, "bfloat16"), ("Zh", 144, "bfloat16"), ("C512", 64, "bfloat16"), ("half", 1, "float32"), ("ki", 768, "int32"), ("ki2", 768, "int32"), ("ki3", 768, "int32"), ("KB", 512, "bfloat16"),
        ("gi", 384, "int32"), ("gi2", 384, "int32"), ("GM", 384, "bfloat16"), ("Ys", 8, "bfloat16"),
        ("vh", 256, "float32"), ("VH", 256, "bfloat16"), ("VL", 256, "bfloat16"), ("V8", 256, "bfloat16")):
    SCRATCH[_n] = ("sbuf", [128, _c], _d)
SCRATCH["PS"] = ("sbuf", [64, 512], "int32")
SCRATCH["PSf"] = ("sbuf", [64, 512], "float32")
SCRATCH["PT"] = ("sbuf", [64, 512], "float32")
SCRATCH["FT"] = ("sbuf", [128, 512], "bfloat16")
SCRATCH["Rk"] = ("sbuf", [128, 128], "bfloat16")
SCRATCH["irk"] = ("sbuf", [128, 128], "float32")
SCRATCH["mT"] = ("sbuf", [4, 512], "bfloat16")
SCRATCH["SS"] = ("sbuf", [49, 512], "int32")
SCRATCH["SSf"] = ("sbuf", [49, 512], "float32")
SCRATCH["ysb"] = ("sbuf", [8, 960], "float32")
for _k in range(8):
    SCRATCH["b%d" % _k] = ("psum", [128, 512], "float32")
GROUPS = ["dpar", "dsel", "dsl", "dfr", "dsw", "ds0", "ds1", "ds2", "ds3", "doutf", "douts", "doutp"]
SEMAPHORES = ["sV", "sA", "sP", "sG", "rv0", "rv1", "rv2", "ls"] + GROUPS
ENG = ("V", "A", "P", "G", "Y")
MODES = ("SCFF", "SFFF", "SCFF", "SSCF")
CF = {"HM": "FFFA", "f0": 2, "Sg": 2, "fh": 2, "SZ": "G", "CB": "A"}
CY = 0.00095
MODEL = {"cy": 0.00095, "gam": 1.5, "pe": 0.00045, "sem": 0.061, "eps": 0.014, "chunk": 0.0, "vb": 0.86, "vg": 0.45}
SEEDS = [(735020, 2, 0.005), (748862, 0.5, 0.01), (94243, 1, 0.005), (242009, 1, 0.005), (385449, 0.5, 0.005), (234413, 1, 0.005), (385998, 4, 0.005),
         (526160, 0.5, 0.005), (749604, 2, 0.005), (130020, 1, 0.01), (86384, 0.5, 0.005)]


def spread(n):
    z = np.zeros(n)
    for s, amp, frac in SEEDS:
        g = np.random.default_rng(s)
        z += np.where(g.random(n) < frac, (g.random(n) - 0.5) * amp, 0.0)
    return [float(x) for x in z]


def schedule(ops, succ, M, noise=None):
    n = len(ops)
    d = [o["c"][0] + M["cy"] * (o["c"][1] + o["c"][2] * M["gam"]) + o["c"][3] * M["pe"] for o in ops]
    prio = [0.0] * n
    for k in range(n - 1, -1, -1):
        m = 0.0
        for s in succ[k]:
            if prio[s] > m: m = prio[s]
        prio[k] = d[k] + M["sem"] + ops[k]["b"] - M["chunk"] * (ops[k]["m"] % 10 in (1, 2, 3)) + m + (noise[k % len(noise)] if noise else 0.0)
    left = [len(o["h"] | o["s"]) for o in ops]
    at = [0.0] * n
    free = {e: 0.0 for e in "VAPGYN"}
    where = [o["e"] for o in ops]
    rdy = [k for k in range(n) if left[k] == 0]
    order, end = [], 0.0
    while rdy:
        lo = 1e9
        est = []
        for k in rdy:
            e = where[k]
            if e == "*":
                e = "V" if max(at[k], free["V"]) + M["vb"] < max(at[k], free["A"]) else "A"
                if "gc" in ops[k] and max(at[k], free["G"]) + ops[k]["gc"] < max(at[k], free[e]) + d[k] + M["vg"]: e = "G"
            s = max(at[k], free[e])
            est.append((k, e, s))
            if s < lo: lo = s
        k, e, s = max((x for x in est if x[2] <= lo + M["eps"]), key=lambda x: (prio[x[0]], -x[0]))
        where[k] = e
        if e == "G" and "gc" in ops[k]: d[k] = ops[k]["gc"]
        if e != "N": free[e] = s + (0.1 if ops[k]["g"] is not None and ops[k]["g"] != "send" else d[k])
        order.append(k)
        rdy.remove(k)
        end = max(end, s + d[k])
        for x in succ[k]:
            left[x] -= 1
            at[x] = max(at[x], s + d[k] + M["sem"])
            if left[x] == 0: rdy.append(x)
    return order, where, end


def rank_program(g, core, T, topo):
    rank = T.rank_of(core)
    if rank is None:
        return
    ops = []
    early, mark = [0.0], [0]
    lastw, readers, psum = {}, {}, {}

    def op(eng, fn, r=(), w=(), d=0.1, ps=(), grp=None, bias=0.0):
        k = len(ops)
        hard, soft = set(), set()
        for x in r:
            if x in lastw: hard.add(lastw[x])
        for x in w:
            if x in lastw: hard.add(lastw[x])
            soft |= readers.get(x, set())
        for x in r: readers.setdefault(x, set()).add(k)
        for x in w: lastw[x] = k; readers[x] = set()
        for b in ps:
            runs = psum.setdefault(b, [])
            if not runs or runs[-1][0] != eng or eng == "*": runs.append((eng, []))
            runs[-1][1].append(k)
            if len(runs) > 1: hard |= set(runs[-2][1])
        hard.discard(k); soft.discard(k)
        ops.append({"e": eng, "f": fn, "h": hard, "s": soft - hard, "c": d if isinstance(d, tuple) else (d, 0, 0, 0), "g": grp, "b": bias + early[0], "m": mark[0], "any": eng == "*"})
        return k

    V, A, TE = g.vector, g.scalar, g.tensor

    def vd(n, c=1.0): return (0.02, max(64, n * c), 0, 0)
    def gd(n): return (0.06, 0, n, 0)
    def ad(n): return (0.04, max(64, n), 0, 0)

    def gather(out, win, off, r, w, n):
        op("*", lambda inc, e: inc(V.tensor_copy(out, win.indirect(off)) if e == "V" else A.activation(out, win.indirect(off), AF.Copy)), r, w, gd(n))

    def mg(out, i0, r, w, n):
        def fn(inc, e):
            if e == "G": inc(g.affine_select(out, i0, [[0, n]], OP.is_ge, 0.0, 0, 0))
            else: inc(V.tensor_copy(out, i0) if e == "V" else A.activation(out, i0, AF.Copy))
        k = op("*", fn, r, w, (0.03, max(64, n * 0.75), 0, 0))
        ops[k]["gc"] = 0.17 + 2 * n * CY

    def mv(out, i0, r=(), w=(), n=64, ps=(), h=1.0):
        op("*", lambda inc, e: inc(V.tensor_copy(out, i0) if e == "V" else A.activation(out, i0, AF.Copy)), r, w, ad(n), ps)

    def ts(out, i0, s1, s2, o1, o2=None, r=(), w=(), n=64, ps=(), c=1.0):
        if o2 is None: op("V", lambda inc: inc(V.tensor_scalar(out, i0, s1, None, o1)), r, w, vd(n, c), ps)
        else: op("V", lambda inc: inc(V.tensor_scalar(out, i0, s1, s2, o1, o2)), r, w, vd(n, c), ps)

    def tt(out, i0, i1, o, r=(), w=(), n=64, ps=()):
        op("V", lambda inc: inc(V.tensor_tensor(out, i0, i1, o)), r, w, vd(n, 1.0 if ps else 2.0), ps)

    def cp(out, i0, r=(), w=(), n=64, ps=(), c=1.0):
        op("V", lambda inc: inc(V.tensor_copy(out, i0)), r, w, vd(n, c), ps)

    def act(out, i0, r=(), w=(), n=64, ps=(), f=None, bias=0.0, scale=1.0):
        op("A", lambda inc: inc(A.activation(out, i0, f or AF.Copy, bias=bias, scale=scale)), r, w, ad(n), ps)

    def mm(groups, r=(), w=(), ps=(), n=64):
        def fn(inc):
            for out, prs in groups:
                for j, (a, b) in enumerate(prs):
                    z = TE.matmul(out, a, b, j == 0, j == len(prs) - 1)
                inc(z)
        op("P", fn, r, w, (0.06, 0, 0, sum(len(p) for _, p in groups) * max(64, n)), ps)

    def dma(eng, out, in_, grp, r=(), w=(), d=2.0, bias=0.0):
        q = {"Y": g.sync, "A": g.scalar}[eng]
        op(eng, lambda inc: q.dma_start(out, in_).then_inc(T.sem[grp], 16), r, w, d, grp=grp, bias=bias)

    def iota(out, pat, base, cm, w, n, flag=True):
        if flag: op("G", lambda inc: inc(g.iota(out, pat, base, cm, allow_small_or_imprecise_dtypes=True)), (), w, 0.13 + 2 * n * CY)
        else: op("G", lambda inc: inc(g.iota(out, pat, base, cm)), (), w, 0.13 + 2 * n * CY)

    def fill(ap, c, w, n): op("V", lambda inc: inc(V.memset(ap, c)), (), w, vd(n, 0.5))

    B0 = 3152
    dma("Y", T.sl[:, :], T.sel0[:, :], "dsl", (), ("sl",), bias=50.0)
    dma("Y", T.F[:, 16:B0], T.front[:, :], "dfr", (), ("Fi",), 6.0, 30.0)
    for k in range(8):
        dma("A" if k % 2 else "Y", T.PS[:, 64 * k:64 * k + 64], T.par[16 * k:16 * k + 16, :], "dpar", (), ("PS%d" % k,))
    for k in range(8):
        dma("A" if k % 2 else "Y", T.SS[:, 64 * k:64 * k + 64], T.sel0[k:k + 1, :], "dsel", (), ("SS%d" % k,))
    iota(T.pi[:, :], [[0, 1]], 0, 1, ("pi",), 1, False)
    iota(T.iu[:, :], [[1, 144]], 0, 0, ("iu",), 144)
    iota(T.ib[:, :], [[0, 8], [1, 16]], 0, 0, ("ib",), 128)
    iota(T.irk[:, :], [[0, 32], [1, 4]], 0, 0, ("irk",), 128)
    iota(T.vh[:, :], [[16, 16], [0, 16]], 16, 0, ("vh",), 256)
    iota(T.VL[:, :], [[0, 16], [1, 16]], 0, 0, ("VL",), 256)
    iota(T.V8[:, :], [[0, 256]], 8192, 0, ("V8",), 256)
    iota(T.K63[:, :], [[-1, 64]], 63, 0, ("K63",), 64)
    iota(T.i16[:, :], [[16, 8]], 15, 0, ("i16",), 8)
    iota(T.ki[:, 0:256], [[1, 4], [1, 16], [64, 4]], 0, 0, ("ki0",), 256, False)
    iota(T.ki[:, 256:512], [[5, 4], [37, 16], [320, 4]], 16 if CF["CB"] == "A" else 0, 0, ("ki1",), 256, False)
    iota(T.ki[:, 512:768], [[1, 4], [0, 16], [64, 4]], 0, 0, ("ki2",), 256, False)
    iota(T.gi[:, :], [[1, 6], [0, 16], [4, 4]], 0, 0, ("gi",), 384, False)
    fill(T.F[:, 0:16], 0.0, ("Fz",), 16)
    fill(T.SELw[:, :], 0.0, ("SELw",), 3152)
    early[0] = -6.0
    for k in range(8):
        if CF["SZ"] == "V": fill(T.S[:, 514 * k:514 * k + 514], 0.0, ("Sz%d" % k,), 514)
        else: iota(T.S[:, 514 * k:514 * k + 514], [[0, 514]], 0, 0, ("Sz%d" % k,), 514)
    early[0] = 0.0
    Sz = tuple("Sz%d" % k for k in range(8))
    fill(T.C1[:, 0:16], 0.0, ("C1z",), 16)
    ts(T.pii[:, 0:1], T.pi[:, :], 15, None, OP.bitwise_and, r=("pi",), w=("pii0",))
    ts(T.pii[:, 1:2], T.pi[:, :], 15, 1, OP.bitwise_and, OP.arith_shift_right, r=("pi",), w=("pii1",))
    ts(T.pii[:, 2:3], T.pi[:, :], 3, None, OP.bitwise_and, r=("pi",), w=("pii2",))
    cp(T.pc[:, 0:1], T.pi[:, :], ("pi",), ("pc0",))
    cp(T.pc[:, 1:2], T.pii[:, 0:1], ("pii0",), ("pc1",))
    tt(T.pc[:, 14:15], T.pc[:, 0:1], T.pc[:, 1:2], OP.subtract, ("pc0", "pc1"), ("pc14",))
    ts(T.pc[:, 2:3], T.pc[:, 14:15], 15.0, None, OP.add, r=("pc14",), w=("pc2",))
    ts(T.pc[:, 3:4], T.pc[:, 1:2], 1008.0, None, OP.add, r=("pc1",), w=("pc3",))
    cp(T.pc[:, 4:5], T.pii[:, 1:2], ("pii1",), ("pc4",))
    for k in (1, 2, 3): ts(T.pc[:, 4 + k:5 + k], T.pc[:, 4:5], float(k), None, OP.is_equal, r=("pc4",), w=("pc%d" % (4 + k),))
    for k in (1, 2, 3):
        ts(T.pw[:, 3 + k:4 + k], T.pc[:, 1:2], 8.0, float(k), OP.is_equal, OP.mult, r=("pc1",), w=("pv%d" % k,))
        tt(T.pw[:, k:k + 1], T.pw[:, 3 + k:4 + k], T.pc[:, 4 + k:5 + k], OP.add, ("pv%d" % k, "pc%d" % (4 + k)), ("pw%d" % k,), 64)
    ts(T.pc[:, 8:9], T.pc[:, 1:2], 256.0, None, OP.mult, r=("pc1",), w=("pc8",))
    ts(T.pc[:, 10:11], T.pc[:, 4:5], 3.0, None, OP.is_lt, r=("pc4",), w=("pc10",))
    cp(T.pc[:, 11:12], T.pii[:, 2:3], ("pii2",), ("pc11",))
    ts(T.pc[:, 12:13], T.pc[:, 1:2], 20.0, None, OP.mult, r=("pc1",), w=("pc12",))
    ts(T.pc[:, 13:14], T.pc[:, 1:2], 4.0, None, OP.mult, r=("pc1",), w=("pc13",))
    ts(T.pc[:, 15:16], T.pc[:, 0:1], 2.0, None, OP.add, r=("pc0",), w=("pc15",))
    ts(T.If[:, :], T.iu[:, 0:128], T.pc[:, 0:1], None, OP.is_equal, r=("iu", "pc0"), w=("If",), n=128)
    ts(T.Ib[:, :], T.iu[:, 0:128], T.pc[:, 0:1], None, OP.is_equal, r=("iu", "pc0"), w=("Ib",), n=128)
    ts(T.Z0[:, :], T.iu[:, :], T.pc[:, 2:3], 64.0, OP.is_equal, OP.mult, r=("iu", "pc2"), w=("Z0",), n=144)
    ts(T.Zh[:, :], T.Z0[:, :], 0.5, None, OP.mult, r=("Z0",), w=("Zh",), n=144, c=0.5)
    fill(T.C512[:, :], 512.0, ("C512",), 64)
    fill(T.half[:, :], 0.5, ("half",), 1)
    for k in (1, 2, 3):
        ts(T["Z%d" % k][:, :], T.iu[:, :], T.pc[:, 2:3], T.pw[:, k:k + 1], OP.is_equal, OP.mult, r=("iu", "pc2", "pw%d" % k), w=("Z%d" % k,), n=144)
    ts(T.GA[:, :], T.ib[:, :], T.pc[:, 1:2], None, OP.is_equal, r=("ib", "pc1"), w=("GA",), n=128)
    if CF["CB"] == "A":
        tt(T.GI[:, :], T.GA[:, :], T.Ib[:, :], OP.add, ("GA", "Ib"), ("GI",), 128)
        mv2 = lambda inc: inc(A.activation(T.Ih[:, :], T.Ib[:, :], AF.Copy, scale=0.5))
        op("A", mv2, ("Ib",), ("Ih",), ad(128))
        for j in (0, 1): fill(T.thr[:, j:j + 1], -(16383.5 + 8192 * j), ("thr%d" % j,), 1)
    ts(T.Sh[:, :], T.iu[:, 0:128], T.pc[:, 15:16], T.pc[:, 10:11], OP.is_equal, OP.mult, r=("iu", "pc15", "pc10"), w=("Sh",), n=128)
    ts(T.In[:, :], T.Ib[:, :], -1.0, None, OP.mult, r=("Ib",), w=("In",), n=128, c=0.5)
    for k in range(3):
        ts(T.BI[:, 256 * k:256 * k + 128], T.Ib[:, :], float(B0 + 320 * k), None, OP.mult, r=("Ib",), w=("BIa%d" % k,), n=128, c=0.5)
        ts(T.BI[:, 256 * k + 128:256 * k + 256], T.Ib[:, :], float(B0 + 320 * k + 256), None, OP.mult, r=("Ib",), w=("BIb%d" % k,), n=128, c=0.5)
    ts(T.Rk[:, :], T.irk[:, :], T.pc[:, 11:12], None, OP.is_equal, r=("irk", "pc11"), w=("Rk",), n=128)
    op("V", lambda inc: inc(V.memset(T.Rk[0:64, 64:128], 0.0)), (), ("Rk", "Rky"), vd(64))
    op("V", lambda inc: inc(V.memset(T.Rk[64:128, 0:64], 0.0)), ("Rky",), ("Rk", "Rkz"), vd(64))
    ts(T.Ys[:, :], T.i16[:, :], T.pc[:, 2:3], T.pc[:, 5:6], OP.is_equal, OP.mult, r=("i16", "pc2", "pc5"), w=("Ys",))
    ts(T.ki2[:, 0:256], T.ki[:, 0:256], T.pc[:, 13:14], None, OP.add, r=("ki0", "pc13"), w=("kj0",), n=256)
    ts(T.ki2[:, 256:512], T.ki[:, 256:512], T.pc[:, 12:13], None, OP.add, r=("ki1", "pc12"), w=("kj1",), n=256)
    ts(T.ki3[:, 0:256], T.ki2[:, 0:256], 63, None, OP.bitwise_and, r=("kj0",), w=("kk0",), n=256)
    ts(T.ki3[:, 256:512], T.ki2[:, 256:512], 255, None, OP.bitwise_and, r=("kj1",), w=("kk1",), n=256)
    for r in range(4):
        cp(T.KB[:, 128 * r:128 * r + 64], T.ki3[:, 64 * r:64 * r + 64], ("kk0",), ("KBa%d" % r,))
        cp(T.KB[:, 128 * r + 64:128 * r + 128], T.ki3[:, 256 + 64 * r:320 + 64 * r], ("kk1",), ("KBb%d" % r,))
        ts(T.VT[:, 256 * r + 192:256 * r + 256], T.ki[:, 512 + 64 * r:576 + 64 * r], T.pc[:, 13:14], None, OP.add, r=("ki2", "pc13"), w=("VTi%d" % r,))
    ts(T.gi2[:, :], T.gi[:, :], 15, None, OP.bitwise_and, r=("gi",), w=("gi2",), n=384)
    ts(T.GM[:, :], T.gi2[:, :], T.pc[:, 1:2], None, OP.is_equal, r=("gi2", "pc1"), w=("GM",), n=384)
    op("A", lambda inc: inc(A.activation(T.VH[:, :], T.vh[:, :], AF.Identity, bias=T.pc[:, 8:9])), ("vh", "pc8"), ("VH",), ad(256))
    dma("Y", T.S[0::16, 16:4112], T.VH[:, :], "ds0", ("VH",) + Sz, ("S0",))
    dma("Y", T.S[1::16, 16:4112], T.VL[:, :], "ds0", ("VL",) + Sz, ("S1",))
    dma("Y", T.S[8::16, 16:4112], T.V8[:, :], "ds0", ("V8",) + Sz, ("S8",))
    Sv = Sz
    ts(T.PSf[:, :], T.PS[:, :], 16.0, None, OP.add, r=tuple("PS%d" % k for k in range(8)), w=("PSf",), n=512)
    mm([(T.b6[:, 64 * r:64 * r + 64], [(T.PSf[:, r::4], T.If[0:64, 0:64])]) for r in range(4)], ("PSf", "If"), (), ("b6",), 256)
    cp(T.PL[:, :], T.b6[:, 0:256], (), tuple("PL%d" % r for r in range(4)), 256, ("b6",))
    act(T.Pf[:, :], T.b6[:, 0:256], (), tuple("Pf%d" % r for r in range(4)), 256, ("b6",))
    ts(T.SSf[:, :], T.SS[:, :], 16.0, None, OP.add, r=tuple("SS%d" % k for k in range(8)), w=("SSf",), n=512)
    mm([(T.b5[:, 50 * r:50 * r + 49], [(T.SSf[:, r::4], T.If[0:49, 0:49])]) for r in range(4)], ("SSf", "If"), (), ("b5",), 256)
    for r in range(4): cp(T.LS[:, 50 * r:50 * r + 49], T.b5[:, 50 * r:50 * r + 49], (), ("LS%d" % r,), 64, ("b5",))
    ts(T.slf[:, :], T.sl[:, :], 16.0, None, OP.add, r=("sl",), w=("slf",), n=196)
    cp(T.slh[:, :], T.slf[:, :], ("slf",), ("slh",), 196)
    tt(T.sll[:, :], T.slf[:, :], T.slh[:, :], OP.subtract, ("slf", "slh"), ("sll",), 196)
    dma("Y", T.SELw[2::16, 16:B0], T.slh[:, :], "dsw", ("slh", "SELw"), ("SW2",))
    dma("Y", T.SELw[3::16, 16:B0], T.sll[:, :], "dsw", ("sll", "SELw"), ("SW3",))
    for r in range(4):
        gather(T.C1[:, 16 + r:B0:4], T.SELw[:, :], T.LS[:, 50 * r:50 * r + 49], ("SELw", "SW2", "SW3", "LS%d" % r), ("C1%d" % r,), 784)
    c1 = ("C1z",) + tuple("C1%d" % r for r in range(4))
    for r in range(4):
        gather(T.C2[:, 16 + r:B0:4], T.C1[:, :], T.LS[:, 50 * r:50 * r + 49], c1 + ("LS%d" % r,), ("C2%d" % r,), 784)
    c2 = tuple("C2%d" % r for r in range(4))
    for k in (0, 1):
        dma("Y", T.S[2 + k::16, 16:B0], T.SELw[2 + k::16, 16:B0], "ds1", ("SW2", "SW3") + Sv, ("S%d" % (2 + k),))
    for k in (0, 1):
        dma("Y", T.S[4 + k::16, 16:B0], T.C1[2 + k::16, 16:B0], "ds2", c1 + Sv, ("S%d" % (4 + k),))
    for k in (0, 1):
        dma("Y", T.S[6 + k::16, 16:B0], T.C2[2 + k::16, 16:B0], "ds3", c2 + Sv, ("S%d" % (6 + k),))
    Sr = Sv + tuple("S%d" % k for k in range(9))
    Sv = Sz + ("S0", "S1", "S8")
    Fr = ("Fi", "Fz")

    def z(n, y): return T["Z%s" % n][:, 15 - y:143 - y]

    def key(src, rk, n):
        mm([(T.b0[:, 0:64], [(z(0, y), src[:, y::16]) for y in range(16)] + [(T.Ib[:, :], T.K63[:, :])])], rk + ("Z0", "Ib", "K63"), (), ("b0",))
        for c in range(4):
            op("V", lambda inc, c=c: inc(V.tensor_reduce(T.Mm[:, 8 * n + c:8 * n + c + 1], T.b0[:, c:64:4], AxisListType.X, OP.max)), (), ("Mm%d%d" % (n, c),), vd(64), ("b0",))
        ts(T.mi[:, 8 * n:8 * n + 4], T.Mm[:, 8 * n:8 * n + 4], 63, None, OP.bitwise_and, r=tuple("Mm%d%d" % (n, c) for c in range(4)), w=("mi%d" % n,))
        ts(T.L1[:, 8 * n:8 * n + 4], T.mi[:, 8 * n:8 * n + 4], -16.0, T.pc[:, 3:4], OP.mult, OP.add, r=("mi%d" % n, "pc3"), w=("L1%d" % n,))
        return T.L1[:, 8 * n:8 * n + 4]

    def newsel(n, r, sv, cols, w):
        mm([(T.b7[:, 0:64], [(T.Sh[:, :], T.Sgs[:, 64 * n:64 * n + 64]), (T.Ib[:, :], cols)])], ("Sgs%d" % n, "Sh", "Ib") + Sv, (), ("b7",))
        mv(cols, T.b7[:, 0:64], (), w, 64, ("b7",))

    for t in range(3):
        B = B0 + 320 * t
        win, swin = T.F[:, 0:B], T.S[:, 0:B]
        fin = ()
        for r in range(4):
            q0, q4 = 64 * r, 256 * r
            Q, GP = T["b%d" % (1 + r % 2)], T["b%d" % (3 + r % 2)]
            Qb, GPb = "b%d" % (1 + r % 2), "b%d" % (3 + r % 2)
            R = "%d" % r
            PL, Pf = T.PL[:, q0:q0 + 64], T.Pf[:, q0:q0 + 64]
            f0, f1, Sg = T.f0[:, 1024 * r:1024 * r + 1024], T.f1[:, 1024 * r:1024 * r + 1024], T.Sg[:, 1024 * r:1024 * r + 1024]
            mark[0] = 10 * t + r
            def gath(out, wn, lists, rk, name, parts):
                for b in range(parts):
                    n_ = 1024 // parts
                    gather(out[:, n_ * b:n_ * b + n_], wn, lists[:, n_ // 16 * b:n_ // 16 * (b + 1)], rk,
                           (name + "%d%d" % (r, b),) if parts == 2 else (name + "%d0" % r, name + "%d1" % r), n_)
            gath(f0, win, PL, Fr + ("PL" + R,), "f0", CF["f0"])
            gath(Sg, swin, PL, Sr + ("PL" + R,), "Sg", CF["Sg"])
            f0k, Sgk = ("f0%d0" % r, "f0%d1" % r), ("Sg%d0" % r, "Sg%d1" % r)
            L1 = key(f0, f0k, r)
            gather(T.Gb[:, q0:q0 + 64], f0, L1, f0k + ("L1" + R,), ("Gb" + R,), 64)
            g5 = 512 * r
            mg(T.Gr[:, g5:g5 + 64], T.Gb[:, q0:q0 + 64], ("Gb" + R,), ("Gra" + R,), 64)
            mg(T.Gr[:, g5 + 64:g5 + 128], T.Gb[:, q0:q0 + 64], ("Gb" + R,), ("Grb" + R,), 64)
            mg(T.Gr[:, g5 + 128:g5 + 256], T.Gr[:, g5:g5 + 128], ("Gra" + R, "Grb" + R), ("Grc" + R,), 128)
            mg(T.Gr[:, g5 + 256:g5 + 512], T.Gr[:, g5:g5 + 256], ("Gra" + R, "Grb" + R, "Grc" + R), ("Grd" + R,), 256)
            Gk = tuple("Gr%s%d" % (x, r) for x in "abcd")
            MD = MODES[r]
            mm([(Q[:, 0:64], [(T.If[:, :], Pf)])], ("Pf" + R, "If"), (), (Qb,), 256)
            for h in (1, 2, 3):
                mm([(Q[:, 64 * h:64 * h + 64], [(z(h, y), Sg[:, y::16]) for y in range(16)])], Sgk + ("Z%d" % h,), (), (Qb,))
            for h in (1, 2, 3):
                a = 192 * r + 64 * h - 64
                ts(T.QL[:, a:a + 64], Q[:, 64 * h:64 * h + 64], -8192.0 * h, None, OP.add, w=("QL%d%d" % (r, h),), ps=(Qb,))
            fh = [f0] + [T.f1[:, 4096 * (h - 1) + 1024 * r:4096 * (h - 1) + 1024 * r + 1024] for h in (1, 2, 3)]
            for h in (1, 2, 3):
                a = 192 * r + 64 * h - 64
                if MD[h] != "F": gath(fh[h], win, T.QL[:, a:a + 64], Fr + ("QL%d%d" % (r, h),), "f%d" % h, CF["fh"])
            gather(T.Sgs[:, q0:q0 + 64], Sg, L1, Sgk + ("L1" + R,), ("Sgs" + R,), 64)
            for h in range(4):
                if MD[h] == "C": mm([(GP[:, :], [(T.Ib[:, :], T.Gr[:, g5:g5 + 512])])], Gk + ("Ib",), (), (GPb,), 512)
                for b in (0, 1):
                    le = T.le[:, 4096 * r + 1024 * h + 512 * b:4096 * r + 1024 * h + 512 * b + 512]
                    k = ("le%d%d%d" % (r, h, b),)
                    if MD[h] == "S":
                        D, Db = T["b%d" % (3 + b)], "b%d" % (3 + b)
                        mm([(D[:, :], [(T.In[:, :], fh[h][:, 512 * b:512 * b + 512]), (T.Ib[:, :], T.Gr[:, 512 * r:512 * r + 512])])],
                           ("f%d%d%d" % (h, r, b), "In", "Ib") + Gk, (), (Db,), 512)
                        op("A", lambda inc, le=le, D=D: inc(A.activation(le, D[:, :], AF.Sign, bias=T.half[:, :])), ("half",), k, ad(512), (Db,))
                    elif MD[h] == "C":
                        tt(le, fh[h][:, 512 * b:512 * b + 512], GP[:, :], OP.is_le, ("f%d%d%d" % (h, r, b),), k, 512, (GPb,))
                    else:
                        a = 192 * r + 64 * h - 64 + 32 * b
                        op("V", lambda inc, le=le, a=a, r=r, win=win: inc(V.tensor_tensor(le, win.indirect(T.QL[:, a:a + 32]), T.Gr[:, 512 * r:512 * r + 512], OP.is_le)),
                           Fr + Gk + ("QL%d%d" % (r, h),), k, gd(512))
                lh, sg = 4096 * r + 1024 * h, MD[h] == "S"
                mm([(T.b5[:, 64 * h:64 * h + 64], [(z("h" if sg else 0, y), T.le[:, lh + y:lh + 1024:16]) for y in range(16)] + ([(T.Ib[:, :], T.C512[:, :])] if sg else []))], ("le%d%d0" % (r, h), "le%d%d1" % (r, h), "Z0", "Zh", "C512", "Ib"), (), ("b5",))
            act(T.Rl[:, q4:q4 + 256], T.b5[:, 0:256], (), ("Rl" + R,), 256, ("b5",), AF.Relu, 786432.0, -1024.0)
            tt(Q[:, 256:384], T.Rl[:, q4 + 128:q4 + 256], Q[:, 128:256], OP.add, ("Rl" + R,), ("XP" + Qb,), 128, (Qb,))
            tt(T.X[:, q4:q4 + 128], T.Rl[:, q4:q4 + 128], Q[:, 0:128], OP.add, ("Rl" + R,), ("X" + R,), 128, (Qb,))
            tt(Q[:, 384:448], T.X[:, q4 + 64:q4 + 128], Q[:, 320:384], OP.min, ("X" + R, "XP" + Qb), ("XQ" + Qb,), 64, (Qb,))
            tt(T.X2[:, 128 * r:128 * r + 64], T.X[:, q4:q4 + 64], Q[:, 256:320], OP.min, ("X" + R, "XP" + Qb), ("X2" + R,), 64, (Qb,))
            tt(T.X3[:, q0:q0 + 64], T.X2[:, 128 * r:128 * r + 64], Q[:, 384:448], OP.min, ("X2" + R, "XQ" + Qb), ("X3" + R,), 64, (Qb,))
            ts(T.XI[:, q0:q0 + 64], T.X3[:, q0:q0 + 64], 32768.0, None, OP.min, r=("X3" + R,), w=("XI" + R,))
            ts(T.VT[:, q4:q4 + 64], T.XI[:, q0:q0 + 64], 8191, None, OP.bitwise_and, r=("XI" + R,), w=("VTq" + R,))
            cp(T.QE[:, q0:q0 + 64], T.VT[:, q4:q4 + 64], ("VTq" + R,), ("QE" + R,))
            h5 = 512 * r
            for b in (1, 0):
                hb = h5 + 256 * b
                gather(T.H[:, hb:hb + 256], win, T.QE[:, q0 + 32 + 16 * b:q0 + 48 + 16 * b], Fr + ("QE" + R,), ("H%d%d" % (r, b),), 256)
                if CF["HM"][r] == "A":
                    gather(T.H2[:, hb:hb + 256], win, T.QE[:, q0 + 16 * b:q0 + 16 + 16 * b], Fr + ("QE" + R,), ("H2%d%d" % (r, b),), 256)
                    mm([(T.b7[:, 0:256], [(T.Ib[:, :], T.H[:, hb:hb + 256])])], ("H%d%d" % (r, b), "Ib"), (), ("b7",), 256)
                    tt(T.AC[:, hb:hb + 256], T.H2[:, hb:hb + 256], T.b7[:, 0:256], OP.max, ("H2%d%d" % (r, b),), ("AC%d%d" % (r, b),), 256, ("b7",))
                else: op("V", lambda inc, hb=hb, a=q0 + 16 * b, win=win: inc(V.tensor_tensor(T.AC[:, hb:hb + 256], win.indirect(T.QE[:, a:a + 16]), T.H[:, hb:hb + 256], OP.max)),
                   Fr + ("QE" + R, "H%d%d" % (r, b)), ("AC%d%d" % (r, b),), gd(256))
                if b: mm([(T.b7[:, 256:512], [(T.Ib[:, :], T.AC[:, hb:hb + 256])])], ("AC%d1" % r, "Ib"), (), ("b7",), 256)
            tt(T.b7[:, 128:256], T.AC[:, h5 + 128:h5 + 256], T.b7[:, 384:512], OP.max, ("AC%d0" % r,), ("AP",), 128, ("b7",))
            tt(T.A2[:, q4:q4 + 128], T.AC[:, h5:h5 + 128], T.b7[:, 256:384], OP.max, ("AC%d0" % r,), ("A2" + R,), 128, ("b7",))
            tt(T.b7[:, 64:128], T.A2[:, q4 + 64:q4 + 128], T.b7[:, 192:256], OP.max, ("A2" + R, "AP"), ("AQ",), 64, ("b7",))
            tt(T.A3[:, 128 * r:128 * r + 64], T.A2[:, q4:q4 + 64], T.b7[:, 128:192], OP.max, ("A2" + R, "AP"), ("A3" + R,), 64, ("b7",))
            tt(T.b7[:, 0:64], T.A3[:, 128 * r:128 * r + 64], T.b7[:, 64:128], OP.max, ("A3" + R, "AQ"), ("A4",), 64, ("b7",))
            gm = 64 * (r + t)
            tt(T.A5[:, q0:q0 + 64], T.GM[:, gm:gm + 64], T.b7[:, 0:64], OP.add, ("A4", "GM"), ("A5" + R,), 64, ("b7",))
            fk = "F%d%d" % (t, r)
            if r == 0:
                NF, RV = T["NF%d" % t], T["RV%d" % t]
                ts(NF[:, :], T.A5[:, q0:q0 + 64], 255.0, None, OP.min, r=("A5" + R,), w=("NF%d" % t,), c=0.5)
                dst = T.cores[(rank + 1 + t % 3) % 4]
                src = T.cores[(rank - 1 - t % 3) % 4]
                ne = topo.engines(core, dst)[:8]
                nr = len(topo.engines(src, core)[:8])

                def send(inc, t=t, dst=dst, ne=ne, NF=NF, RV=RV):
                    rid, pid = topo.addr(dst)[:2]
                    g.remote_dma(RV[:, :], NF[:, :], T.sem["rv%d" % t], T.sem["ls"], pid, rid, sum(1 << e for e in ne))
                op("G", send, ("NF%d" % t,), ("sent%d" % t,), 1.5, grp="send")
                op("N", ("rv%d" % t, nr), ("sent%d" % t,), ("RV%d" % t,), 2.5)
                mg(T.F[:, B + r:B + 256:4], NF[:, :], ("NF%d" % t,), (fk,), 64)
            else:
                ts(T.F[:, B + r:B + 256:4], T.A5[:, q0:q0 + 64], 255.0, None, OP.min, r=("A5" + R,), w=(fk,), c=0.5)
            newsel(r, r, None, T.S[:, B + r:B + 256:4], ("T%d%d" % (t, r),))
            m4 = 8 * r
            cp(T.mb[:, m4:m4 + 4], T.mi[:, m4:m4 + 4], ("mi" + R,), ("mb" + R,))
            mm([(T.b6[0:4, 256:384], [(T.mb[:, m4:m4 + 4], T.Ib[:, :])])], ("mb" + R, "Ib"), (), ("b6",), 128)
            mv(T.mT[:, 128 * r:128 * r + 128], T.b6[0:4, 256:384], (), ("mT" + R,), 128, ("b6",))
            mm([(T.b6[:, 0:64], [(T.mT[:, 128 * r:128 * r + 128], T.Rk[0:4, 0:64]), (T.In[:, :], T.K63[:, :])])], ("mT" + R, "Rk", "In", "K63"), (), ("b6",))
            ts(T.MK[:, q4 + 192:q4 + 256], T.b6[:, 0:64], 0.0, None, OP.is_equal, w=("MKs" + R,), ps=("b6",))
            ts(T.MK[:, q4:q4 + 64], T.X3[:, q0:q0 + 64], 8192.0, None, OP.is_ge, r=("X3" + R,), w=("MKn" + R,))
            ts(T.MK[:, q4 + 128:q4 + 192], T.X3[:, q0:q0 + 64], 32768.0, None, OP.is_ge, r=("X3" + R,), w=("MKr" + R,))
            if CF["CB"] == "V":
                ts(T.CI[:, q0:q0 + 64], T.XI[:, q0:q0 + 64], 13, None, OP.arith_shift_right, r=("XI" + R,), w=("CI" + R,))
                cp(T.cb[:, q0:q0 + 64], T.CI[:, q0:q0 + 64], ("CI" + R,), ("cb" + R,))
            else:
                for j in (0, 1):
                    op("A", lambda inc, j=j, q0=q0: inc(A.activation(T.sA[:, 2 * q0 + 64 * j:2 * q0 + 64 * j + 64], T.X3[:, q0:q0 + 64], AF.Sign, bias=T.thr[:, j:j + 1])),
                       ("X3" + R, "thr%d" % j), ("sA%d%d" % (r, j),), ad(64))
            tt(T.MK[:, q4 + 64:q4 + 128], T.MK[:, q4:q4 + 64], T.MK[:, q4 + 192:q4 + 256], OP.is_equal, ("MKn" + R, "MKs" + R), ("MK0" + R,), 64)
            red, cb = T.MK[:, q4 + 128:q4 + 192], T.cb[:, q0:q0 + 64]
            if CF["CB"] == "V":
                mm([(T.b6[0:64, 0:128], [(red, T.GA[:, :])]), (T.b6[64:128, 0:128], [(red, T.GA[:, :]), (cb, T.Ib[:, :])])], ("MKr" + R, "cb" + R, "GA", "Ib"), (), ("b6",), 128)
            else:
                mm([(T.b6[0:64, 0:128], [(red, T.GA[:, :])]),
                    (T.b6[64:128, 0:128], [(red, T.GI[:, :]), (T.MK[:, q4:q4 + 64], T.Ib[:, :])] + [(T.sA[:, 2 * q0 + 64 * j:2 * q0 + 64 * j + 64], T.Ih[:, :]) for j in (0, 1)])],
                   ("MKr" + R, "MKn" + R, "sA%d0" % r, "sA%d1" % r, "GA", "GI", "Ib", "Ih"), (), ("b6",), 128)
            kb = 128 * r
            mv(T.FT[:, kb:kb + 128], T.b6[:, 0:128], (), ("FT" + R,), 128, ("b6",))
            mm([(T.b6[:, 256:384], [(T.FT[:, kb:kb + 128], T.Rk[:, :]), (T.Ib[:, :], T.KB[:, kb:kb + 128])])],
               ("FT" + R, "Rk", "Rkz", "Ib", "KBa" + R, "KBb" + R), (), ("b6",), 128)
            cp(T.RI[:, kb:kb + 128], T.b6[:, 256:384], (), ("RI" + R,), 128, ("b6",))
            ts(T.VT[:, q4 + 64:q4 + 128], T.RI[:, kb:kb + 64], 63, None, OP.bitwise_and, r=("RI" + R,), w=("VTb" + R,))
            ts(T.VT[:, q4 + 128:q4 + 192], T.RI[:, kb + 64:kb + 128], 255, None, OP.bitwise_and, r=("RI" + R,), w=("VTa" + R,))
            mk = ("MKn" + R, "MK0" + R, "MKr" + R, "MKs" + R)
            mm([(T.b6[:, 0:256], [(T.Ib[:, :], T.MK[:, q4:q4 + 256])])], mk + ("Ib",), (), ("b6",), 256)
            tt(T.PRD[:, q0:q0 + 64], T.VT[:, q4:q4 + 64], T.b6[:, 0:64], OP.mult, ("VTq" + R,), ("PRD" + R,), 64, ("b6",))
            tt(T.PRB[:, q4:q4 + 192], T.VT[:, q4 + 64:q4 + 256], T.b6[:, 64:256], OP.mult, ("VTb" + R, "VTa" + R, "VTi" + R), ("PRB" + R,), 192, ("b6",))
            BA, BB = T.BI[:, 256 * t:256 * t + 128], T.BI[:, 256 * t + 128:256 * t + 256]
            mm([(T.b6[:, 384:448], [(BA, T.MK[:, q4 + 128:q4 + 192]), (BA, T.MK[:, q4 + 192:q4 + 256]), (BB, T.MK[:, q4 + 64:q4 + 128])]
                 + [(T.Ib[:, :], T.PRB[:, q4 + 64 * j:q4 + 64 * j + 64]) for j in range(3)] + [(T.If[:, :], T.PRD[:, q0:q0 + 64])])],
               mk + ("PRD" + R, "PRB" + R, "If", "Ib", "BIa%d" % t, "BIb%d" % t), (), ("b6",), 92)
            mv(Pf, T.b6[:, 384:448], (), ("Pf" + R,), 64, ("b6",))
            if t < 2:
                cp(PL, T.b6[:, 384:448], (), ("PL" + R,), 64, ("b6",))
            else:
                mm([(T.b6[0:64, 0:128], [(Pf, T.If[:, :])])], ("Pf" + R, "If"), (), ("b6",), 512)
                act(T.PT[:, r::4], T.b6[0:64, 0:128], (), ("PT" + R,), 128, ("b6",), bias=-16.0)
        mark[0] = 10 * t + 4
        rv = ("RV%d" % t,)
        mm([(T.b3[:, 64 * k:64 * k + 64], [(T.Ib[:, :], RV[:, :])]) for k in range(8)], rv + ("Ib",), (), ("b3",))
        for b in (0, 1):
            tt(T.ler[:, 512 * b:512 * b + 512], T.f0[:, 512 * b:512 * b + 512], T.b3[:, :], OP.is_le, ("f00%d" % b,), ("ler%d" % b,), 512, ("b3",))
        mg(T.F[:, B + 256:B + 320], RV[:, :], rv, ("F%d4" % t,), 64)
        L4 = key(T.ler[:, :], ("ler0", "ler1"), 4)
        gather(T.Sgs[:, 256:320], T.Sg[:, 0:1024], L4, ("Sg00", "Sg01", "L14"), ("Sgs4",), 64)
        newsel(4, None, None, T.S[:, B + 256:B + 320], ("T%d4" % t,))
        fn = tuple("F%d%d" % (t, r) for r in range(5))
        sn = tuple("T%d%d" % (t, r) for r in range(5))
        Fr += fn
        Sr += sn
        dma("Y", T.yf[:, 320 * t:320 * t + 320], T.F[:, B:B + 320], "doutf", fn)
        mm([(T.b7[0:8, 0:320], [(T.Ys[:, :], T.S[:, B:B + 320])])], sn + ("Ys",), (), ("b7",), 320)
        act(T.ysb[:, 320 * t:320 * t + 320], T.b7[0:8, 0:320], (), ("ysb%d" % t,), 320, ("b7",), bias=-16.0)
        dma("Y", T.ys[:, 320 * t:320 * t + 320], T.ysb[:, 320 * t:320 * t + 320], "douts", ("ysb%d" % t,))
    for k in range(8):
        dma("YA"[k % 2], T.yp[16 * k:16 * k + 16, :], T.PT[:, 64 * k:64 * k + 64], "doutp", tuple("PT%d" % r for r in range(4)))

    n = len(ops)
    succ = [[] for _ in range(n)]
    for k, o in enumerate(ops):
        for d in o["h"] | o["s"]: succ[d].append(k)
    order, where, _ = schedule(ops, succ, MODEL, spread(n))
    for k in range(n): ops[k]["e"] = where[k]
    sem = {e: T.sem["s" + e] for e in "VAPG"}
    queue = {"V": g.vector, "A": g.scalar, "P": g.tensor, "G": g, "Y": g.sync}
    gtot = {}
    for o in ops:
        if o["g"] and o["g"] != "send": gtot[o["g"]] = gtot.get(o["g"], 0) + 16
    cnt = {e: 0 for e in "VAPG"}
    done = {}
    seen = {e: {} for e in ENG}
    know = {}
    for k in order:
        o = ops[k]
        e = o["e"]
        need = {}
        for d in o["h"] | o["s"]:
            if d in o["s"] and ops[d]["e"] == e and o["g"] is None and ops[d]["g"] is None: continue
            if e == "N": continue
            for kk, v in (done[d],):
                if kk is not None: need[kk] = max(need.get(kk, 0), v)
        if e == "N":
            done[k] = (o["f"][0], o["f"][1])
            know[k] = {}
            continue
        hit = {}
        for kk in need:
            if seen[e].get(kk, 0) < need[kk]: hit[kk] = need[kk]
        for d in o["h"] | o["s"]:
            if done[d][0] in hit and done[d][1] <= hit[done[d][0]]:
                for kk, v in know[d].items():
                    if kk in hit and kk != done[d][0] and v >= hit[kk]: del hit[kk]
        for kk, v in hit.items():
            queue[e].wait_ge(T.sem[kk], int(v))
            seen[e][kk] = v
        for d in o["h"] | o["s"]:
            if d in o["s"] and ops[d]["e"] == e: continue
            for kk, v in know[d].items(): seen[e][kk] = max(seen[e].get(kk, 0), v)
        if o["g"] is not None:
            o["f"](None)
            done[k] = (None, 0) if o["g"] == "send" else (o["g"], gtot[o["g"]])
            know[k] = dict(seen[e])
        else:
            def inc(i, e=e):
                cnt[e] += 1
                i.then_inc(sem[e], 1)
            if o["any"]: o["f"](inc, e)
            else: o["f"](inc)
            done[k] = ("s" + e, cnt[e])
            know[k] = dict(seen[e])
            know[k]["s" + e] = cnt[e]
    for e in "VAPG": g.wait_ge(sem[e], cnt[e])
    for q in gtot: g.wait_ge(T.sem[q], gtot[q])
    nl = 0
    for t in range(3):
        nl += len(topo.engines(core, T.cores[(rank + 1 + t % 3) % 4])[:8])
        g.wait_ge(T.sem["rv%d" % t], len(topo.engines(T.cores[(rank - 1 - t % 3) % 4], core)[:8]))
    g.wait_ge(T.sem["ls"], nl)
